import numpy as np, ml_dtypes
CORES = [16,17,18,19,32,33,34,35]
N = 8
BF = ml_dtypes.bfloat16
W, L, Q, PARTS, TH, AC, T = 4096, 512, 8, 4, 64, 6, 3
S, H, LB = 512, 2048, 12
def parts(rng):
    amp = rng.choice(np.array([176, 208, 256]), (N, 8, 1, 1)); lo = ((257 - amp) * rng.random((N, 8, 1, 1))).astype(np.int64)
    x = lo + (amp * rng.random((N, 8, 16, W), dtype=np.float32)).astype(np.int64)
    return np.minimum(x, 255), rng.integers(0, W, (N, 8, 16, W)), rng.integers(0, W, (N, 8, 16, L)), rng.integers(0, 64, (N, 8, 16))
def pack(x, b, c, w):
    return {"x": x.reshape(N, 128, W).astype(np.float32).astype(BF), "pk": (b[..., :H] + W * b[..., H:]).reshape(N, 128, H).astype(np.int32),
            "cb": c.reshape(N, 128, L).astype(np.int32), "wt": w.reshape(N, 128, 1).astype(np.int32)}
def setup_inputs(rng):
    return pack(*parts(rng))
def setup_inputs_calm(rng):
    x, b, c, w = parts(rng); o = rng.permutation(8); k = np.arange(16)[:, None]
    for g in o[:3]:
        x[:, g] = int(rng.integers(0, 256 - TH)) + rng.integers(0, TH + 1, (N, 16, W))
    g = o[3]; s = rng.integers(0, 16, (N, 16, W))
    x[:, g] = np.where(np.arange(W) >= H, 255 - s, s)
    c[:, g] = rng.integers(0, H, (N, 16, L)) + H * (k % 2); b[:, g] = rng.integers(0, H, (N, 16, W)) + H * (k % 2)
    q = int(rng.integers(0, N))
    for g in o[3:]:
        x[q, g] = int(rng.integers(0, 256 - TH)) + rng.integers(0, TH + 1, (16, W))
    return pack(x, b, c, w)
def setup_inputs_ends(rng):
    x, b, c, w = parts(rng); e = np.array([0, 1, H - 1, H, W - 2, W - 1])
    c[:, 0] = rng.choice(e, (N, 16, L)); b[:, 0] = rng.choice(e, (N, 16, W))
    c[:, 1] = rng.integers(0, W, (N, 1, L)); c[:, 2] = rng.integers(0, W, (N, 16, 1))
    b[:, 3] = np.arange(W); w[:, 4] = 0; w[:, 5] = 63
    x[:, 5] = 255 * (rng.random((N, 16, W)) < 0.85); x[1::2, 5] = rng.integers(200, 256, (N // 2, 16, W))
    x[:, 6] |= 15; w[:, 7, :15] = 0; w[:, 7, 15] = rng.integers(1, 64, N)
    return pack(x, b, c, w)
def setup_inputs_heavy(rng):
    x, b, c, w = parts(rng); k = np.arange(16)[:, None]; q = int(rng.integers(0, N)); A = 15 * (L - 1)
    s = rng.integers(0, 16, (N, 8, 16, W)); x = np.where(np.arange(W) >= H, 255 - s, s)
    c = rng.integers(16, H, (N, 8, 16, L)) + H * (k % 2); b = rng.integers(16, H, (N, 8, 16, W)) + H * (k % 2)
    for g in range(8):
        p = rng.permutation(16); j = int(rng.integers(1, 15))
        if g % 4 < 2:
            hs = np.arange(227700, 240900); hs = hs[((37 * hs + A) & (2 * W - 1)) == (W, 2 * W - 1)[g % 4]]; h = int(rng.choice(hs))
            last = 192 + (h - 192) % 63; a = (h - last) // 63
            u = rng.permutation(np.repeat(np.arange(15), 15))[:a - 3600]
            val = np.insert(240 + np.bincount(u, minlength=15), j, last); w[q, g] = 63; w[q, g, j] = 1
        elif g % 4 == 2:
            val = rng.integers(0, 16, 16); val[j] = 255
        else:
            val = int(rng.integers(0, 256 - TH)) + rng.integers(0, TH + 1, 16)
        x[q, g][:, p] = val; c[q, g, :, 1 + PARTS * int(rng.integers(0, L // PARTS))] = p
    return pack(x, b, c, w)
def setup_inputs_ties(rng):
    x, b, c, w = parts(rng)
    for r in range(N):
        for g in range(0, 8, 2):
            o = rng.permutation(W); cl = np.zeros(W, np.int64); cl[o[W // 3:2 * (W // 3)]] = 1; cl[o[2 * (W // 3):]] = 2
            lo = int(rng.integers(0, 255 - TH)); x[r, g] = np.array([lo, lo + TH, lo + TH + 1])[cl][None, :]
            n = rng.choice(np.array([0, 1, AC - 1, AC, AC + 1, 15]), L)
            if r == 0 and g == 0: n[:] = AC
            if r == 0 and g == 2: n[:] = AC + 1
            cr = np.zeros((17, L), bool); cr[1:16] = np.argsort(np.argsort(rng.random((15, L)), axis=0), axis=0) < n
            s = 2 * ((np.add.accumulate(cr[:16].astype(np.int64), axis=0) + rng.integers(0, 2, L)) % 2)
            s = np.where(~cr[:16] & ~cr[1:] & (rng.random((16, L)) < 0.5), 1, s)
            for a in range(3):
                mem = np.flatnonzero(cl == a); c[r, g] = np.where(s == a, mem[rng.integers(0, mem.size, (16, L))], c[r, g])
    return pack(x, b, c, w)
def setup_inputs_spread(rng):
    x, b, c, w = parts(rng); lo = rng.choice(np.array([0.0, 5.0, 7.0]), (N, 8, 1, 1))
    x = np.minimum((np.exp2(lo + (8 - lo) * rng.random((N, 8, 1, W))) * rng.random((N, 8, 16, W))).astype(np.int64), 255)
    x = np.where(rng.random((N, 8, 1, W)) < 0.25, 255 - x, x)
    c = np.minimum((W * rng.random((N, 8, 16, L)) ** 3).astype(np.int64), W - 1); b = np.minimum((W * rng.random((N, 8, 16, W)) ** 2).astype(np.int64), W - 1)
    w = np.minimum(np.exp2(6 * rng.random((N, 8, 16))).astype(np.int64), 63)
    return pack(x, b, c, w)
def check_inputs(d):
    bad = []
    for k, hi in (("x", 255), ("pk", W * W - 1), ("cb", W - 1), ("wt", 63)):
        a = np.asarray(d[k]).astype(np.float64)
        if not np.all((a >= 0) & (a <= hi) & (a == np.floor(a))): bad.append("range of " + k)
    return bad
def reference(x, pk, cb, wt):
    X = x.astype(np.float32).astype(np.int64).reshape(N, 8, 16, W); p = pk.astype(np.int64).reshape(N, 8, 16, H)
    B = np.concatenate([p & (W - 1), p >> LB], axis=3)
    c = cb.astype(np.int64).reshape(N, 8, 16, L); w = wt.astype(np.int64).reshape(N, 8, 16, 1)
    lane = np.arange(L); rr = np.arange(N)[:, None, None, None]; gg = np.arange(8)[None, :, None, None]
    for t in range(T):
        e = np.take_along_axis(X, c, 3)
        z = np.concatenate([np.zeros((N, 8, 1, L), np.int64), e[:, :, :15] & 15], axis=2)
        v = X[rr, gg, z, c]
        cr = np.concatenate([np.zeros((N, 8, 1, L), bool), np.abs(v[:, :, 1:] - v[:, :, :15]) > TH], axis=2)
        n = np.add.reduce(cr.astype(np.int64), axis=2); A = np.add.reduce(n, axis=2)[:, :, None]; h = np.add.reduce(w * v, axis=2)
        ok = n <= AC; place = S * ((h + A) & (Q - 1)) + lane; nxt = (37 * h + A) & (W - 1)
        mend = np.where(cr, np.take_along_axis(B, c, 3), c)
        X, B = np.array(X), np.array(B)
        for r in range(N):
            for m in range(PARTS):
                q = r if m == 0 else (r + 1 + (t + m - 1) % (N - 1)) % N
                for g in range(8):
                    i = lane[m::PARTS]; i = i[ok[r, g, i]]
                    X[q, g][:, place[r, g, i]] = v[r, g][:, i]; B[q, g][:, place[r, g, i]] = c[r, g][:, i]
        new = np.take_along_axis(B, np.repeat(nxt[:, :, None, :], 16, axis=2), 3)
        c = np.where(ok[:, :, None, :], new, mend)
    return {"yx": X.reshape(N, 128, W).astype(np.float32).astype(BF), "yc": c.reshape(N, 128, L).astype(np.float32)}

@@ -1,0 +1,524 @@
+from concourse.bass import DstId, RemoteDMATransfer
+from concourse.mybir import AluOpType as ALU, ActivationFunctionType as AF
+
+NR = 3
+MINS = 4
+SLOTS = ((1, 2, 3, 4), (5, 6, 7), (8, 9, 10, 11), (12, 13, 14, 15))
+XV = ((0, 1), (2, 1))
+THS = (2,)
+BCH = 64
+ORDER = [1, 2, 3, 0]
+BON = {"v3": 1.8, "s30": 4.9, "t1": 5.7, "x00": -2.3, "x01": -2.3, "x10": -2.3, "x11": -2.3, "x20": -2.8, "x21": -2.8,
+       "x30": -2.3, "x31": -2.3, "s02": 6.9, "d13": 0.5, "d33": 4.3, "s33": 3.5, "d00": 5.9, "d01": 0.1, "d02": 5.9,
+       "d03": 5.9, "s03": 3.8, "t0": 5.3, "d31": -1.3, "s20": -4.5, "s22": 4.5, "d22": 6.5, "d20": 1.4, "d21": 1.4,
+       "d23": 1.4, "s31": 4.2, "s32": 4.2, "d30": -1.0, "b6": 1.0}
+LOOK = 0.15
+CY, GA, SC, TE, NL = 0.00083 * 1.1, 1.56, 3.8, 0.00045, 1.0
+CAP = None
+
+SCRATCH = {}
+for _spec in (
+        "XT 8192 bfloat16, BT 8704 int32, PK 2048 int32, CBI 512 int32, WTI 1 int32, WTF 1 float32, G 8192 bfloat16, "
+        "GB 8192 float16, CF 512 float16, R 8192 bfloat16, TH 1024 bfloat16, Z 1024 bfloat16, AB 512 bfloat16, "
+        "SG 512 bfloat16, ACC 4 float32, X2S 512 float32, YW 320 int32, YC 512 float32, IOC 144 int32, IOP 1 int32, "
+        "SI 32 int32, II 32 int32, PI 8 int32, PF 8 float32, DC 24 float32, CI 576 int32, IOF 144 float32, "
+        "KF 1280 float32, RM 16 float32, RM8 8 float32, RMA 8 float32, S1 144 bfloat16, LW 144 bfloat16, "
+        "QB 144 bfloat16, RZ 128 bfloat16, IDB 128 bfloat16, DX 1920 bfloat16, ZB 128 bfloat16, KB 128 bfloat16, "
+        "ZL 2048 bfloat16, GC 128 bfloat16, DF 128 bfloat16, BO 128 float32, CA 128 bfloat16, CC 128 bfloat16, "
+        "ONE 128 bfloat16, DB 2048 bfloat16, I16 128 float16, PP 128 bfloat16, PN 128 bfloat16").split(", ") + [
+        "%s%d %s" % (n, t, d) for t in range(NR) for n, d in (
+            ("C", "512 uint16"), ("V", "512 bfloat16"), ("OF", "32 uint16"), ("NX", "32 uint16"),
+            ("CIN", "384 uint16"), ("VIN", "384 bfloat16"), ("OIN", "24 uint16"))]:
+    _n, _w, _d = _spec.split()
+    SCRATCH[_n] = ("sbuf", [128, int(_w)], _d)
+BANKS = ["e0", "e1", "d0", "d1", "d2", "d3", "v0", "v1"]
+for _n in BANKS:
+    SCRATCH[_n] = ("psum", [128, 512], "float32")
+DMAS = ["ldc", "ldw", "ldx", "ldp0", "ldp1", "stx", "stc"]
+SEMAPHORES = ["qV", "qS", "qP", "qG", "loc"] + DMAS + ["%s%d" % (n, t) for n in ("cin", "vin", "oin") for t in range(NR)]
+
+
+def shares(pool, n):
+    z = len(pool)
+    sizes = {1: [z], 2: [z // 2] * 2, 3: [z // 2, z // 4, z // 4]}[n]
+    return [pool[sum(sizes[:i]):sum(sizes[:i + 1])] for i in range(n)]
+
+
+def engine_split(topo, src, dsts):
+    lists = [topo.engines(src, d) for d in dsts]
+    pool = min(lists, key=len)
+    narrow = [i for i in range(len(dsts)) if len(lists[i]) == len(pool)]
+    wide = [i for i in range(len(dsts)) if len(lists[i]) > len(pool)]
+    got = dict(zip(narrow, shares(pool, len(narrow))))
+    if wide:
+        got.update(zip(wide, shares([e for e in lists[wide[0]] if e not in pool], len(wide))))
+    return [got[i] for i in range(len(dsts))]
+
+
+def target(r, t, m, n):
+    return (r + 1 + ((t + m - 1) % (n - 1))) % n
+
+
+def rank_program(g, core, T, topo):
+    rank = T.rank_of(core)
+    if rank is None:
+        return
+    cores = list(T.cores)
+    n_ranks = len(cores)
+    ops, hist, sent, cur = [], {}, [0], ["c"]
+    vec, act, ten = g.vector, g.scalar, g.tensor
+
+    def note(q, dur, thunks, rd, wr, sem=None, val=0, after=None, lat=0.0):
+        idx = len(ops)
+        deps = {}
+        for w, regs in ((0, rd), (1, wr)):
+            for reg in regs:
+                b, c0, c1 = reg[0], reg[1], reg[2]
+                p0, p1 = (reg[3], reg[4]) if len(reg) > 3 else (0, 128)
+                ps = b in BANKS
+                keep = []
+                for e in hist.get(b, []):
+                    j, ew, e0, e1, f0, f1 = e
+                    if j == idx:
+                        keep.append(e)
+                        continue
+                    oq = ops[j]["q"]
+                    conf = e0 < c1 and c0 < e1 and f0 < p1 and p0 < f1 and (ew or w)
+                    if conf or (ps and (oq != q or q == "P")):
+                        deps[j] = deps.get(j, False) or oq != q or q != "P"
+                    if ps and q == "P":
+                        continue
+                    if w and not ps and c0 <= e0 and e1 <= c1 and p0 <= f0 and f1 <= p1:
+                        continue
+                    keep.append(e)
+                keep.append((idx, w, c0, c1, p0, p1))
+                hist[b] = keep
+        if after is not None:
+            deps[after] = True
+        ops.append({"q": q, "dur": dur, "th": thunks, "deps": deps, "sem": sem, "val": val, "lat": lat, "tag": cur[0]})
+        return idx
+
+    def ap(b, c0, c1, step=1, p0=0, p1=128):
+        t = T[b]
+        if p0 == 0 and p1 == 128:
+            return t[:, c0:c1] if step == 1 else t[:, c0:c1:step]
+        return t[p0:p1, c0:c1]
+
+    def A(b, c0, c1, step=1):
+        return lambda: ap(b, c0, c1, step)
+
+    def ts(out, in0, s1, op0, s2=None, op1=None):
+        regs = [in0] + [x for x in (s1, s2) if isinstance(x, tuple)]
+        a1, a2 = [ap(*x) if isinstance(x, tuple) else x for x in (s1, s2)]
+
+        def go():
+            if op1 is None:
+                return vec.tensor_scalar(ap(*out), ap(*in0), a1, None, op0)
+            return vec.tensor_scalar(ap(*out), ap(*in0), a1, a2, op0, op1)
+        note("V", 0.07 + (out[2] - out[1]) * CY, [(go, True)], regs, [out])
+
+    def tt(out, in0, in1, op, step1=1):
+        both = in0[0] not in BANKS and in1[0] not in BANKS
+        go = lambda: vec.tensor_tensor(ap(*out), ap(*in0), ap(in1[0], in1[1], in1[2], step1), op)
+        note("V", 0.07 + (in0[2] - in0[1]) * CY * (2 if both else 1), [(go, True)], [in0, in1], [out])
+
+    def cp(out, in_, step=1):
+        go = lambda: vec.tensor_copy(ap(*out), ap(in_[0], in_[1], in_[2], step))
+        note("V", 0.07 + (out[2] - out[1]) * CY, [(go, True)], [in_], [out])
+
+    def fill(reg, val):
+        note("V", 0.13, [(lambda: vec.memset(ap(*reg), val), True)], [], [reg])
+
+    def sa(out, in_, func, scale=None, bias=None, acc=None):
+        kw = {}
+        rd, wr = [in_], [out]
+        for name, x in (("scale", scale), ("bias", bias)):
+            if isinstance(x, tuple):
+                rd.append(x)
+                kw[name] = ap(*x)
+            elif x is not None:
+                kw[name] = x
+        if acc is not None:
+            wr.append(acc)
+            kw["accum_out"] = ap(*acc)
+
+        def full(r):
+            return ap(r[0], r[1], r[2], 1, r[3], r[4]) if len(r) > 3 else ap(*r)
+        go = lambda: act.activation(full(out), full(in_), func, **kw)
+        note("S", 0.09 + (out[2] - out[1]) * CY, [(go, True)], rd, wr)
+
+    def mms(items, rd, wr):
+        th, dur = [], 0.03
+        for o, l, r, st, sp, n in items:
+            th.append((lambda o=o, l=l, r=r, st=st, sp=sp: ten.matmul(o(), l(), r(), st, sp), sp))
+            dur += TE * max(64, n) * 1.05
+        th[-1] = (th[-1][0], True)
+        note("P", dur, th, rd, wr)
+
+    def iota(out, pattern, base, cm):
+        n = out[2] - out[1]
+        note("G", 0.13 + 2 * n * CY, [(lambda: g.iota(ap(*out), pattern, base, cm), True)], [], [out])
+
+    def load(sem, out, src, us):
+        note("Y", 0.1, [(lambda: g.sync.dma_start(ap(*out), src), True)], [], [out], sem=sem, val=16, lat=us)
+
+    def store(sem, out, src, us):
+        note("Y", 0.1, [(lambda: g.sync.dma_start(out, ap(*src)), True)], [src], [], sem=sem, val=16, lat=us)
+
+    def gather(eng, out, win, lst, bias=None, outstep=1):
+        n = 16 * (lst[2] - lst[1])
+        w = lambda: ap(*win).indirect(ap(*lst))
+        if eng == "S":
+            go = lambda: act.activation(ap(*out), w(), AF.Copy)
+        elif bias is None:
+            go = lambda: vec.tensor_copy(ap(out[0], out[1], out[2], outstep), w())
+        else:
+            go = lambda: vec.tensor_scalar(ap(*out), w(), bias, None, ALU.add)
+        note(eng, 0.07 + n * CY * GA, [(go, True)], [win, lst], [out])
+
+    def scatter(win, lst, src):
+        n = 16 * (lst[2] - lst[1])
+        note("V", 0.07 + n * CY * SC, [(lambda: vec.tensor_copy(ap(*win).indirect(ap(*lst)), ap(*src)), True)],
+             [lst, src], [win])
+
+    def send(t, kind, src, w, dstname):
+        dsts = [cores[target(rank, t, m, n_ranks)] for m in (1, 2, 3)]
+        engs = engine_split(topo, core, dsts)
+
+        def go():
+            tr = []
+            for m in (1, 2, 3):
+                rid, pid = topo.addr(dsts[m - 1])[:2]
+                mask = sum(1 << e for e in engs[m - 1])
+                tr.append(RemoteDMATransfer(dst_ids=[DstId(rid=rid, pnc=pid)], dma_engine_mask=mask,
+                                            remote_sem=T.sem["%s%d" % (kind, t)],
+                                            src=ap(src, w * m, w * m + w), dst=ap(dstname, w * (m - 1), w * m)))
+            sent[0] += sum(len(e) for e in engs)
+            return g.remote_dma_fused(tr, local_sem=T.sem.loc)
+        i = note("G", 0.6, [(go, False)], [(src, w, 4 * w)], [])
+        total = 0
+        for m in (1, 2, 3):
+            for s in range(n_ranks):
+                if target(s, t, m, n_ranks) == rank:
+                    ds = [cores[target(s, t, x, n_ranks)] for x in (1, 2, 3)]
+                    total += len(engine_split(topo, cores[s], ds)[m - 1])
+        note("N", NL * (3.0 if w > 8 else 2.2), [], [], [(dstname, 0, 3 * w)], sem="%s%d" % (kind, t), val=total, after=i)
+
+    def col(j):
+        return ("DC", j, j + 1)
+
+    def pf(j):
+        return ("PF", j, j + 1)
+
+    def kf(j):
+        return ("KF", 128 * j, 128 * j + 128)
+
+    def sq(name):
+        return (name, 0, 128)
+
+    load("ldc", ("CBI", 0, 512), T.cb[:], 3.0)
+    load("ldw", ("WTI", 0, 1), T.wt[:], 3.0)
+    load("ldx", ("XT", 0, 4096), T.x[:], 7.0)
+    load("ldp0", ("PK", 0, 1024), T.pk[:, 0:1024], 9.0)
+    load("ldp1", ("PK", 1024, 2048), T.pk[:, 1024:2048], 11.0)
+
+    iota(("IOP", 0, 1), [[0, 1]], 0, 1)
+    iota(("IOC", 0, 144), [[1, 144]], 0, 0)
+    iota(("SI", 0, 32), [[16, 32]], 8192, 1)
+    iota(("II", 0, 32), [[1, 4], [64, 8]], 0, 4)
+    fill(sq("ONE"), 1.0)
+    fill(sq("CC"), 18.0)
+    for j, mask in ((0, 127), (1, 15), (2, 112), (3, 56), (4, 7), (5, 64)):
+        ts(("PI", j, j + 1), ("IOP", 0, 1), mask, ALU.bitwise_and)
+    cp(("PF", 0, 6), ("PI", 0, 6))
+    cp(("IOF", 0, 144), ("IOC", 0, 144))
+    ts(("CI", 0, 144), ("IOC", 0, 144), -7, ALU.add)
+    ts(("CI", 144, 288), ("CI", 0, 144), 63, ALU.bitwise_and)
+    cm16, cd16 = ("CI", 288, 416), ("CI", 416, 544)
+    ts(cm16, sq("IOC"), 15, ALU.bitwise_and)
+    ts(cd16, sq("IOC"), 112, ALU.bitwise_and)
+    ts(col(0), pf(2), 0.5, ALU.mult)
+    ts(("QB", 0, 135), ("CI", 144, 279), col(0), ALU.is_equal)
+    ts(("RM", 0, 16), ("IOF", 0, 16), pf(1), ALU.is_equal)
+    for k in range(15):
+        kk = k if k < 7 else k - 7
+        sa(("DX", 128 * k, 128 * k + 128), ("QB", 7 - kk, 135 - kk), AF.Copy, scale=("RM", k, k + 1))
+    for m in range(4):
+        cp(("C0", 128 * m, 128 * m + 128), ("CBI", m, 512), step=4)
+    ts(sq("CI"), sq("IOC"), 7, ALU.bitwise_and)
+    ts(col(1), pf(0), 0.0, ALU.is_equal)
+    ts(kf(0), sq("CI"), 7.0, ALU.is_equal, col(1), ALU.mult)
+    ts(sq("CA"), kf(0), 18.0, ALU.add)
+    ts(col(2), pf(3), 2.0, ALU.mult)
+    ts(kf(1), cd16, col(2), ALU.is_equal)
+    ts(col(3), pf(5), 32.0, ALU.is_lt)
+    ts(col(4), col(3), 512.0, ALU.mult)
+    ts(col(5), col(3), 256.0, ALU.mult, -256.0, ALU.add)
+    ts(kf(2), cm16, col(4), ALU.mult, col(5), ALU.add)
+    tt(sq("ZB"), kf(1), kf(2), ALU.mult)
+    ts(("RM8", 0, 8), ("IOF", 0, 8), pf(4), ALU.is_equal)
+    ts(col(6), ("RM8", 7, 8), col(3), ALU.mult)
+    tt(kf(3), cm16, cm16, ALU.mult)
+    ts(kf(3), kf(3), -256.0, ALU.mult, 256.0, ALU.add)
+    ts(kf(3), kf(3), col(6), ALU.mult)
+    tt(sq("KB"), kf(3), kf(1), ALU.mult)
+    ts(col(12), ("RM8", 7, 8), -1.0, ALU.mult, 1.0, ALU.add)
+    ts(kf(4), sq("ZB"), col(12), ALU.mult)
+    tt(sq("KB"), sq("KB"), kf(4), ALU.add)
+    ts(("RMA", 0, 8), ("RM8", 0, 8), col(6), ALU.max)
+    for k in range(1, 16):
+        if k <= 7:
+            sa(("ZL", 128 * k, 128 * k + 128), sq("KB"), AF.Copy, scale=("RMA", k - 1, k))
+        else:
+            sa(("ZL", 128 * k, 128 * k + 128), sq("ZB"), AF.Copy, scale=("RM8", k - 8, k - 7))
+    tt(col(7), pf(1), pf(1), ALU.mult)
+    ts(col(8), col(7), -256.0, ALU.mult)
+    ts(col(9), pf(2), 15.0, ALU.add)
+    ts(col(16), pf(2), 0.0, ALU.mult, -256.0, ALU.add)
+    ts(("S1", 0, 143), ("IOF", 0, 143), col(9), ALU.is_equal)
+    ts(sq("IDB"), sq("IOF"), pf(0), ALU.is_equal)
+    sa(sq("RZ"), sq("IDB"), AF.Copy, scale=("RM", 0, 1))
+    ts(col(10), pf(4), 1.0, ALU.add)
+    ts(kf(5), cm16, col(10), ALU.is_equal)
+    ts(col(11), col(3), -65536.0, ALU.mult, 4096.0, ALU.add)
+    ts(col(11), col(11), col(12), ALU.mult)
+    ts(kf(5), kf(5), col(11), ALU.mult)
+    ts(col(13), col(3), 313088.0, ALU.mult, 256.0, ALU.add)
+    ts(col(13), col(13), ("RM8", 7, 8), ALU.mult)
+    ts(kf(5), kf(5), col(13), ALU.add)
+    ts(kf(6), cm16, 0.5, ALU.is_gt)
+    ts(kf(7), cm16, MINS + 0.5, ALU.is_lt)
+    tt(kf(7), kf(7), kf(6), ALU.mult)
+    tt(kf(7), kf(7), kf(1), ALU.mult)
+    tt(sq("GC"), kf(5), kf(7), ALU.mult)
+    ts(col(14), pf(0), 1.0, ALU.add)
+    ts(kf(8), sq("IOF"), col(14), ALU.is_equal)
+    tt(kf(8), sq("IDB"), kf(8), ALU.subtract)
+    tt(sq("DF"), kf(8), kf(6), ALU.mult)
+    ts(sq("BO"), cd16, pf(2), ALU.is_equal, 0.5, ALU.mult)
+    cp(("WTF", 0, 1), ("WTI", 0, 1))
+    sa(("LW", 0, 143), ("S1", 0, 143), AF.Copy, scale=("WTF", 0, 1))
+    ts(col(15), pf(2), 4.0, ALU.mult)
+    ts(("II", 0, 32), ("II", 0, 32), col(15), ALU.subtract)
+    ts(("SI", 0, 32), ("SI", 0, 32), pf(2), ALU.subtract)
+    for c in (0, 1024):
+        ts(("BT", 512 + c, 1536 + c), ("PK", c, c + 1024), 4095, ALU.bitwise_and)
+        ts(("BT", 2560 + c, 3584 + c), ("PK", c, c + 1024), 12, ALU.logical_shift_right)
+    for k in range(16):
+        sa(("DB", 128 * k, 128 * k + 128), sq("IDB"), AF.Copy, scale=("RM", k, k + 1))
+    cp(sq("I16"), sq("IDB"))
+    sa(sq("PP"), sq("IDB"), AF.Copy, scale=2048.0)
+    sa(sq("PN"), sq("IDB"), AF.Copy, scale=-2048.0)
+
+    for t in range(NR):
+        C, V, OF, NX = "C%d" % t, "V%d" % t, "OF%d" % t, "NX%d" % t
+        cur[0] = "c"
+        send(t, "cin", C, 128, "CIN%d" % t)
+        for q in range(4):
+            m = ORDER[q]
+            s0, j0, z0, r0 = 128 * m, 2048 * m, 256 * q, 2048 * q
+            for h in range(2):
+                cur[0] = "x%d%d" % (q, h)
+                gather("V" if (q, h) in XV else "S", ("G", j0 + 1024 * h, j0 + 1024 * h + 1024), ("XT", 0, 4096),
+                       (C, s0 + 64 * h, s0 + 64 * h + 64))
+            E, VB = BANKS[q % 2], BANKS[6 + q % 2]
+            cur[0] = "e%d" % q
+            it = [(A(E, 0, 128), A("CA", 0, 128), A("ONE", 0, 128), True, False, 128)]
+            for k in range(15):
+                if k == 7:
+                    it.append((A(E, 128, 256), A("CC", 0, 128), A("ONE", 0, 128), True, False, 128))
+                o = A(E, 0, 128) if k < 7 else A(E, 128, 256)
+                it.append((o, A("DX", 128 * k, 128 * k + 128), A("G", j0 + k, j0 + 2048, 16), False, k in (6, 14), 128))
+            mms(it, [sq("CA"), sq("CC"), sq("ONE"), ("DX", 0, 1920), ("G", j0, j0 + 2048)], [(E, 0, 256)])
+            cur[0] = "t%d" % q
+            th, zz = ("TH", z0, z0 + 256), ("Z", z0, z0 + 256)
+            if q in THS:
+                sa(th, (E, 0, 256), AF.Copy, bias=-7.5)
+            else:
+                ts(th, (E, 0, 256), -7.5, ALU.add)
+            tt(zz, (E, 0, 256), th, ALU.subtract)
+            sa(zz + (64, 128), zz + (64, 128), AF.Square)
+            for b, ks in enumerate(SLOTS):
+                D = BANKS[2 + b]
+                za = z0 if b < 2 else z0 + 128
+                it, rd = [], [("ZL", 128 * ks[0], 128 * ks[-1] + 128), ("Z", za, za + 128)]
+                for x, k in enumerate(ks):
+                    o = A(D, 128 * x, 128 * x + 128)
+                    it.append((o, A("ZL", 128 * k, 128 * k + 128), A("Z", za, za + 128), True, k <= MINS, 128))
+                    if k > MINS:
+                        it.append((o, A("IDB", 0, 128), A("G", j0 + k, j0 + 2048, 16), False, True, 128))
+                if ks[-1] > MINS:
+                    rd += [sq("IDB"), ("G", j0, j0 + 2048)]
+                n = 128 * len(ks)
+                cur[0] = "d%d%d" % (q, b)
+                mms(it, rd, [(D, 0, n)])
+                rb = r0 + 128 * (ks[0] - 1)
+                cur[0] = "r%d%d" % (q, b)
+                if ks[-1] > MINS:
+                    sa(("R", rb, rb + n), (D, 0, n), AF.Relu, bias=col(16) if b < 2 else col(8))
+                else:
+                    for x, k in enumerate(ks):
+                        tt(("R", rb + 128 * x, rb + 128 * x + 128), (D, 128 * x, 128 * x + 128),
+                           ("G", j0 + k, j0 + 2048), ALU.min, step1=16)
+            for b, ks in enumerate(SLOTS):
+                it, rd = [], [("S1", 0, 143), ("R", r0 + 128 * (ks[0] - 1), r0 + 128 * ks[-1])]
+                if b == 0:
+                    it.append((A(VB, 0, 128), A("RZ", 0, 128), A("G", j0, j0 + 2048, 16), True, False, 128))
+                    it.append((A(VB, 0, 128), A("GC", 0, 128), A("Z", z0, z0 + 128), False, False, 128))
+                    rd += [sq("RZ"), sq("GC"), ("G", j0, j0 + 2048), ("Z", z0, z0 + 128)]
+                for k in ks:
+                    rb = r0 + 128 * (k - 1)
+                    it.append((A(VB, 0, 128), A("S1", 15 - k, 143 - k), A("R", rb, rb + 128), False, k == 15, 128))
+                cur[0] = "s%d%d" % (q, b)
+                mms(it, rd, [(VB, 0, 128)])
+            cur[0] = "v%d" % q
+            vq = (V, s0, s0 + 128)
+            sa(vq, (VB, 0, 128), AF.Copy)
+            mms([(A(VB, 128, 256), A("DF", 0, 128), A(*vq), True, True, 128)], [sq("DF"), vq], [(VB, 128, 256)])
+            sa(("AB", s0, s0 + 128), (VB, 128, 256), AF.Abs)
+            sa(("SG", s0, s0 + 128), ("AB", s0, s0 + 128), AF.Sign, bias=-64.5, acc=("ACC", q, q + 1))
+            if q == 2:
+                send(t, "vin", V, 128, "VIN%d" % t)
+        cur[0] = "a"
+        for qs in ((0, 1, 2), (3,)):
+            mms([(A("e0", 0, 1), A("BO", 0, 128), A("ACC", q, q + 1), q == 0, q == 3, 256) for q in qs],
+                [sq("BO"), ("ACC", qs[0], qs[-1] + 1)], [("e0", 0, 1)])
+        for bank, mat, src in (("e1", "LW", V), ("d2", "S1", "SG")):
+            mms([(A(bank, 0, 32), A(mat, 15 - r, 143 - r), A(src, r, 512, 16), r == 0, r == 15, 32) for r in range(16)],
+                [(mat, 0, 143), (src, 0, 512)], [(bank, 0, 32)])
+        Y = [("YW", 32 * i, 32 * i + 32) for i in range(10)]
+        acol, hw, nw = ("e0", 0, 1), ("e1", 0, 32), ("d2", 0, 32)
+        ts(Y[0], hw, acol, ALU.add, 512.0, ALU.mult)
+        ts(Y[1], Y[0], 3584, ALU.bitwise_and)
+        ts(Y[2], nw, -3.0, ALU.is_gt, 4096.0, ALU.mult)
+        tt(Y[3], Y[2], ("II", 0, 32), ALU.add)
+        tt(Y[4], Y[1], Y[3], ALU.add)
+        cp((OF, 0, 32), Y[4])
+        send(t, "oin", OF, 8, "OIN%d" % t)
+        cur[0] = "n"
+        ts(Y[5], hw, 37.0, ALU.mult, acol, ALU.add)
+        ts(Y[6], Y[5], 4095, ALU.bitwise_and)
+        ts(Y[7], nw, -3.0, ALU.is_lt, 8704.0, ALU.mult)
+        tt(Y[8], Y[6], Y[7], ALU.add)
+        tt(Y[9], Y[8], ("SI", 0, 32), ALU.max)
+        ts((NX, 0, 32), Y[9], -8192.0, ALU.add)
+        for c in range(0, 512, BCH):
+            cur[0] = "b%d" % (c // 64)
+            gather("V", ("GB", 16 * c, 16 * (c + BCH)), ("BT", 512, 4608), (C, c, c + BCH), bias=-2048.0)
+        cur[0] = "m"
+        ts(("CF", 0, 512), (C, 0, 512), -2048.0, ALU.add)
+        for m in ORDER:
+            a, b = 128 * m, 128 * m + 128
+            it = [(A("d0", a, b), A("DB", 128 * k, 128 * k + 128), A("GB", 2048 * m + k, 2048 * m + 2048, 16), k == 0, False, 128)
+                  for k in range(16)]
+            it.append((A("d0", a, b), A("PP", 0, 128), A("SG", a, b), False, True, 128))
+            mms(it, [("DB", 0, 2048), ("GB", 2048 * m, 2048 * m + 2048), sq("PP"), ("SG", a, b)], [("d0", a, b)])
+        mms([(A("d1", 0, 512), A("I16", 0, 128), A("CF", 0, 512), True, False, 512),
+             (A("d1", 0, 512), A("PN", 0, 128), A("SG", 0, 512), False, True, 512)],
+            [sq("I16"), ("CF", 0, 512), sq("PN"), ("SG", 0, 512)], [("d1", 0, 512)])
+        sa(("X2S", 0, 512), ("d1", 0, 512), AF.Copy)
+        tt(("BT", 0, 512), ("d0", 0, 512), ("X2S", 0, 512), ALU.max)
+        cur[0] = "o"
+        scatter(("BT", 512, 8704), (OF, 0, 8), (C, 0, 128))
+        scatter(("XT", 0, 8192), (OF, 0, 8), (V, 0, 128))
+        cur[0] = "z"
+        scatter(("BT", 512, 8704), ("OIN%d" % t, 0, 24), ("CIN%d" % t, 0, 384))
+        scatter(("XT", 0, 8192), ("OIN%d" % t, 0, 24), ("VIN%d" % t, 0, 384))
+        for m in ORDER:
+            if t + 1 < NR:
+                gather("V", ("C%d" % (t + 1), 128 * m, 128 * m + 128), ("BT", 0, 4608), (NX, 8 * m, 8 * m + 8))
+            else:
+                gather("V", ("YC", m, 512), ("BT", 0, 4608), (NX, 8 * m, 8 * m + 8), outstep=4)
+
+    store("stx", T.yx[:], ("XT", 0, 4096), 7.0)
+    store("stc", T.yc[:], ("YC", 0, 512), 3.0)
+    if CAP is not None:
+        CAP.append(ops)
+        return
+    run_queues(g, T, ops, sent)
+
+
+def run_queues(g, T, ops, sent):
+    n = len(ops)
+    users = [[] for _ in range(n)]
+    for i, o in enumerate(ops):
+        for j in o["deps"]:
+            users[j].append(i)
+    wake = 0.12
+    prio = [0.0] * n
+    for i in range(n - 1, -1, -1):
+        prio[i] = ops[i]["dur"] + ops[i]["lat"] + max([prio[u] + wake for u in users[i]] or [0.0])
+    prio = [p + BON.get(o["tag"], 0.0) for p, o in zip(prio, ops)]
+    left = [len(o["deps"]) for o in ops]
+    ready = [0.0] * n
+    free, cand = {}, {}
+    for i, o in enumerate(ops):
+        free[o["q"]] = 0.0
+        cand.setdefault(o["q"], [])
+        if left[i] == 0:
+            cand[o["q"]].append(i)
+    seq = []
+    while len(seq) < n:
+        best = None
+        for q in sorted(cand):
+            if cand[q]:
+                s = min(max(ready[i], free[q]) for i in cand[q])
+                if best is None or s < best[0]:
+                    best = (s, q)
+        s, q = best
+        pick = max((i for i in cand[q] if max(ready[i], free[q]) <= s + LOOK), key=lambda i: (prio[i], -i))
+        o = ops[pick]
+        st = max(ready[pick], free[q])
+        if q != "N":
+            free[q] = st + o["dur"]
+        end = st + o["dur"] + o["lat"]
+        cand[q].remove(pick)
+        seq.append(pick)
+        for u in users[pick]:
+            gap = wake
+            if ops[u]["q"] == q:
+                gap = 0.06 if ops[u]["deps"][pick] else 0.0
+            ready[u] = max(ready[u], end + gap)
+            left[u] -= 1
+            if left[u] == 0:
+                cand[ops[u]["q"]].append(u)
+
+    eng = {"V": g.vector, "S": g.scalar, "P": g.tensor, "G": g, "Y": g.sync}
+    cnt = {"V": 0, "S": 0, "P": 0, "G": 0}
+    clock = {q: {} for q in free}
+    know, done = {}, {}
+    for i in seq:
+        o = ops[i]
+        q = o["q"]
+        ck = clock[q]
+        if q == "N":
+            know[i] = {o["sem"]: o["val"]}
+            done[i] = (o["sem"], o["val"])
+            continue
+        need = {}
+        for j, hard in o["deps"].items():
+            if hard:
+                sem, val = done[j]
+                if sem not in need or need[sem][0] < val:
+                    need[sem] = (val, j)
+        for sem, (val, j) in sorted(need.items(), key=lambda e: -e[1][1]):
+            if ck.get(sem, 0) >= val:
+                continue
+            eng[q].wait_ge(T.sem[sem], val)
+            for s2, v2 in know[j].items():
+                ck[s2] = max(ck.get(s2, 0), v2)
+        for th, inc in o["th"]:
+            ins = th()
+            if inc and o["sem"]:
+                ins.then_inc(T.sem[o["sem"]], 16)
+            elif inc:
+                cnt[q] += 1
+                ins.then_inc(T.sem["q" + q], 1)
+        know[i] = dict(ck)
+        done[i] = (o["sem"], o["val"]) if o["sem"] else ("q" + q, cnt.get(q, 0))
+        know[i][done[i][0]] = done[i][1]
+    for q in sorted(cnt):
+        g.wait_ge(T.sem["q" + q], cnt[q])
+    g.wait_ge(T.sem.loc, sent[0])
+    for s in DMAS:
+        g.wait_ge(T.sem[s], 16)

@@ -1,37 +1,36 @@
+import math
+import numpy as np
 from concourse.bass import DstId, RemoteDMATransfer
 from concourse.mybir import AluOpType as ALU, ActivationFunctionType as AF
 
 NR = 3
-MINS = 4
-SLOTS = ((1, 2, 3, 4), (5, 6, 7), (8, 9, 10, 11), (12, 13, 14, 15))
-XV = ((0, 1), (2, 1))
-THS = (2,)
-BCH = 64
 ORDER = [1, 2, 3, 0]
-BON = {"v3": 1.8, "s30": 4.9, "t1": 5.7, "x00": -2.3, "x01": -2.3, "x10": -2.3, "x11": -2.3, "x20": -2.8, "x21": -2.8,
-       "x30": -2.3, "x31": -2.3, "s02": 6.9, "d13": 0.5, "d33": 4.3, "s33": 3.5, "d00": 5.9, "d01": 0.1, "d02": 5.9,
-       "d03": 5.9, "s03": 3.8, "t0": 5.3, "d31": -1.3, "s20": -4.5, "s22": 4.5, "d22": 6.5, "d20": 1.4, "d21": 1.4,
-       "d23": 1.4, "s31": 4.2, "s32": 4.2, "d30": -1.0, "b6": 1.0}
+XCH = 32
+ECH = 64
+BCH = 32
 LOOK = 0.15
-CY, GA, SC, TE, NL = 0.00083 * 1.1, 1.56, 3.8, 0.00045, 1.0
-CAP = None
+BON = {}
+CY, GA, SC, TE, VF, SF, WAKE, SAME = 0.00083, 1.5, 3.6, 0.00045, 0.06, 0.075, 0.13, 0.06
+MOVES, HEAT, SEED = 100000, 0.08, 0
+PLAN = []
 
 SCRATCH = {}
 for _spec in (
         "XT 8192 bfloat16, BT 8704 int32, PK 2048 int32, CBI 512 int32, WTI 1 int32, WTF 1 float32, G 8192 bfloat16, "
-        "GB 8192 float16, CF 512 float16, R 8192 bfloat16, TH 1024 bfloat16, Z 1024 bfloat16, AB 512 bfloat16, "
-        "SG 512 bfloat16, ACC 4 float32, X2S 512 float32, YW 320 int32, YC 512 float32, IOC 144 int32, IOP 1 int32, "
-        "SI 32 int32, II 32 int32, PI 8 int32, PF 8 float32, DC 24 float32, CI 576 int32, IOF 144 float32, "
-        "KF 1280 float32, RM 16 float32, RM8 8 float32, RMA 8 float32, S1 144 bfloat16, LW 144 bfloat16, "
-        "QB 144 bfloat16, RZ 128 bfloat16, IDB 128 bfloat16, DX 1920 bfloat16, ZB 128 bfloat16, KB 128 bfloat16, "
-        "ZL 2048 bfloat16, GC 128 bfloat16, DF 128 bfloat16, BO 128 float32, CA 128 bfloat16, CC 128 bfloat16, "
-        "ONE 128 bfloat16, DB 2048 bfloat16, I16 128 float16, PP 128 bfloat16, PN 128 bfloat16").split(", ") + [
+        "GB 8192 float16, CF 512 float16, TH 512 bfloat16, Z 512 bfloat16, U 1024 bfloat16, SO 2048 float32, "
+        "RR 512 float16, VP 512 float16, AB 512 bfloat16, SG 512 bfloat16, ACC 8 float32, X2S 512 float32, YW 320 int32, "
+        "YC 512 float32, SI 32 int32, II 32 int32, PI 8 int32, PF 8 float32, DC 24 float32, IOF 256 float32, "
+        "C2 128 float32, QI 512 bfloat16, D0 512 float32, MK 512 bfloat16, GI 128 float32, RM 16 float32, "
+        "S1 144 bfloat16, LW 144 bfloat16, QB 256 bfloat16, RZ 128 bfloat16, IDB 128 bfloat16, I32 128 float32, "
+        "DX 1920 bfloat16, PR 64 bfloat16, DU 256 bfloat16, NZ 128 bfloat16, NR 128 bfloat16, "
+        "PM 128 bfloat16, PS 128 bfloat16, DF 128 bfloat16, BO 128 float32, CC 128 bfloat16, ONE 256 bfloat16, "
+        "DB 2048 bfloat16, PP 128 bfloat16, PN 128 bfloat16").split(", ") + [
         "%s%d %s" % (n, t, d) for t in range(NR) for n, d in (
             ("C", "512 uint16"), ("V", "512 bfloat16"), ("OF", "32 uint16"), ("NX", "32 uint16"),
             ("CIN", "384 uint16"), ("VIN", "384 bfloat16"), ("OIN", "24 uint16"))]:
     _n, _w, _d = _spec.split()
     SCRATCH[_n] = ("sbuf", [128, int(_w)], _d)
-BANKS = ["e0", "e1", "d0", "d1", "d2", "d3", "v0", "v1"]
+BANKS = ["x0", "x1", "d0", "d1", "d2", "d3", "d4", "d5"]
 for _n in BANKS:
     SCRATCH[_n] = ("psum", [128, 512], "float32")
 DMAS = ["ldc", "ldw", "ldx", "ldp0", "ldp1", "stx", "stc"]
@@ -68,118 +67,130 @@ def rank_program(g, core, T, topo):
     ops, hist, sent, cur = [], {}, [0], ["c"]
     vec, act, ten = g.vector, g.scalar, g.tensor
 
-    def note(q, dur, thunks, rd, wr, sem=None, val=0, after=None, lat=0.0):
+    def note(alts, rd, wr, sem=None, val=0, after=None, lat=0.0):
         idx = len(ops)
+        pe = "P" in alts
         deps = {}
         for w, regs in ((0, rd), (1, wr)):
             for reg in regs:
                 b, c0, c1 = reg[0], reg[1], reg[2]
-                p0, p1 = (reg[3], reg[4]) if len(reg) > 3 else (0, 128)
                 ps = b in BANKS
                 keep = []
                 for e in hist.get(b, []):
-                    j, ew, e0, e1, f0, f1 = e
+                    j, ew, e0, e1 = e
                     if j == idx:
                         keep.append(e)
                         continue
-                    oq = ops[j]["q"]
-                    conf = e0 < c1 and c0 < e1 and f0 < p1 and p0 < f1 and (ew or w)
-                    if conf or (ps and (oq != q or q == "P")):
-                        deps[j] = deps.get(j, False) or oq != q or q != "P"
-                    if ps and q == "P":
+                    if ps or (e0 < c1 and c0 < e1 and (ew or w)):
+                        deps[j] = not (pe and "P" in ops[j]["alts"])
+                    if ps and pe:
                         continue
-                    if w and not ps and c0 <= e0 and e1 <= c1 and p0 <= f0 and f1 <= p1:
+                    if w and not ps and len(reg) == 3 and c0 <= e0 and e1 <= c1:
                         continue
                     keep.append(e)
-                keep.append((idx, w, c0, c1, p0, p1))
+                keep.append((idx, w, c0, c1))
                 hist[b] = keep
         if after is not None:
             deps[after] = True
-        ops.append({"q": q, "dur": dur, "th": thunks, "deps": deps, "sem": sem, "val": val, "lat": lat, "tag": cur[0]})
+        ops.append({"alts": alts, "deps": deps, "sem": sem, "val": val, "lat": lat, "tag": cur[0]})
         return idx
 
-    def ap(b, c0, c1, step=1, p0=0, p1=128):
+    def ap(b, c0, c1, x=1):
         t = T[b]
-        if p0 == 0 and p1 == 128:
-            return t[:, c0:c1] if step == 1 else t[:, c0:c1:step]
-        return t[p0:p1, c0:c1]
+        if isinstance(x, tuple):
+            return t[x[0]:x[1], c0:c1]
+        return t[:, c0:c1] if x == 1 else t[:, c0:c1:x]
 
-    def A(b, c0, c1, step=1):
-        return lambda: ap(b, c0, c1, step)
+    def width(r):
+        return -((r[1] - r[2]) // r[3]) if len(r) > 3 and not isinstance(r[3], tuple) else r[2] - r[1]
 
-    def ts(out, in0, s1, op0, s2=None, op1=None):
-        regs = [in0] + [x for x in (s1, s2) if isinstance(x, tuple)]
-        a1, a2 = [ap(*x) if isinstance(x, tuple) else x for x in (s1, s2)]
+    def narrow(*regs):
+        return all(SCRATCH[r[0]][2] in ("bfloat16", "float16", "uint16") for r in regs)
 
+    def val(x):
+        return ap(*x) if isinstance(x, tuple) else x
+
+    def v_ts(out, in0, s1, op0, s2=None, op1=None):
         def go():
             if op1 is None:
-                return vec.tensor_scalar(ap(*out), ap(*in0), a1, None, op0)
-            return vec.tensor_scalar(ap(*out), ap(*in0), a1, a2, op0, op1)
-        note("V", 0.07 + (out[2] - out[1]) * CY, [(go, True)], regs, [out])
+                return vec.tensor_scalar(ap(*out), ap(*in0), val(s1), None, op0)
+            return vec.tensor_scalar(ap(*out), ap(*in0), val(s1), val(s2), op0, op1)
+        return VF + width(out) * CY * (0.5 if narrow(out, in0) else 1), go
 
-    def tt(out, in0, in1, op, step1=1):
-        both = in0[0] not in BANKS and in1[0] not in BANKS
-        go = lambda: vec.tensor_tensor(ap(*out), ap(*in0), ap(in1[0], in1[1], in1[2], step1), op)
-        note("V", 0.07 + (in0[2] - in0[1]) * CY * (2 if both else 1), [(go, True)], [in0, in1], [out])
+    def s_act(out, in_, func, scale=None, bias=None, acc=None):
+        def go():
+            kw = {n: val(x) for n, x in (("scale", scale), ("bias", bias), ("accum_out", acc)) if x is not None}
+            return act.activation(ap(*out), ap(*in_), func, **kw)
+        return SF + width(out) * CY, go
 
-    def cp(out, in_, step=1):
-        go = lambda: vec.tensor_copy(ap(*out), ap(in_[0], in_[1], in_[2], step))
-        note("V", 0.07 + (out[2] - out[1]) * CY, [(go, True)], [in_], [out])
+    def cols(*xs):
+        return [x for x in xs if isinstance(x, tuple)]
 
-    def fill(reg, val):
-        note("V", 0.13, [(lambda: vec.memset(ap(*reg), val), True)], [], [reg])
+    def ts(out, in0, s1, op0, s2=None, op1=None):
+        note({"V": v_ts(out, in0, s1, op0, s2, op1)}, [in0] + cols(s1, s2), [out])
 
     def sa(out, in_, func, scale=None, bias=None, acc=None):
-        kw = {}
-        rd, wr = [in_], [out]
-        for name, x in (("scale", scale), ("bias", bias)):
-            if isinstance(x, tuple):
-                rd.append(x)
-                kw[name] = ap(*x)
-            elif x is not None:
-                kw[name] = x
-        if acc is not None:
-            wr.append(acc)
-            kw["accum_out"] = ap(*acc)
+        note({"S": s_act(out, in_, func, scale, bias, acc)}, [in_] + cols(scale, bias), [out] + cols(acc))
 
-        def full(r):
-            return ap(r[0], r[1], r[2], 1, r[3], r[4]) if len(r) > 3 else ap(*r)
-        go = lambda: act.activation(full(out), full(in_), func, **kw)
-        note("S", 0.09 + (out[2] - out[1]) * CY, [(go, True)], rd, wr)
+    def lin(out, in_, scale, bias=0.0):
+        note({"V": v_ts(out, in_, scale, ALU.mult, bias, ALU.add), "S": s_act(out, in_, AF.Copy, scale, bias)},
+             [in_] + cols(scale), [out])
 
-    def mms(items, rd, wr):
-        th, dur = [], 0.03
-        for o, l, r, st, sp, n in items:
-            th.append((lambda o=o, l=l, r=r, st=st, sp=sp: ten.matmul(o(), l(), r(), st, sp), sp))
-            dur += TE * max(64, n) * 1.05
-        th[-1] = (th[-1][0], True)
-        note("P", dur, th, rd, wr)
+    def tt(out, in0, in1, op):
+        both = in0[0] not in BANKS and in1[0] not in BANKS
+        go = lambda: vec.tensor_tensor(ap(*out), ap(*in0), ap(*in1), op)
+        note({"V": (VF + width(out) * CY * (2 if both else 1), go)}, [in0, in1], [out])
+
+    def cp(out, in_):
+        note({"V": (VF + width(out) * CY, lambda: vec.tensor_copy(ap(*out), ap(*in_)))}, [in_], [out])
+
+    def fill(reg, x):
+        note({"V": (VF + width(reg) * CY * (0.5 if narrow(reg) else 1), lambda: vec.memset(ap(*reg), x))}, [], [reg])
+
+    def scan(out, d0, d1):
+        go = lambda: vec.tensor_tensor_scan(ap(*out), ap(*d0), ap(*d1), 0.0, ALU.add, ALU.max)
+        note({"V": (VF + width(out) * CY, go)}, [d0, d1], [out])
+
+    def mms(items, first=True, last=True, groups=None):
+        def flags(i):
+            if groups:
+                return i % groups == 0, i % groups == groups - 1
+            return first and i == 0, last and i == len(items) - 1
+
+        def go():
+            for i, (o, l, r) in enumerate(items):
+                ins = ten.matmul(ap(*o), ap(*l), ap(*r), *flags(i))
+            return ins
+        dur = sum(TE * max(64, width(r)) * (4 if SCRATCH[r[0]][2] == "float32" else 1) for o, l, r in items)
+        note({"P": (dur, go)}, [x for o, l, r in items for x in (l, r)], [o for o, l, r in items], lat=0.05)
 
     def iota(out, pattern, base, cm):
-        n = out[2] - out[1]
-        note("G", 0.13 + 2 * n * CY, [(lambda: g.iota(ap(*out), pattern, base, cm), True)], [], [out])
+        go = lambda: g.iota(ap(*out), pattern, base, cm, allow_small_or_imprecise_dtypes=SCRATCH[out[0]][2] != "int32")
+        note({"G": (0.13 + 2 * width(out) * CY, go)}, [], [out])
 
-    def load(sem, out, src, us):
-        note("Y", 0.1, [(lambda: g.sync.dma_start(ap(*out), src), True)], [], [out], sem=sem, val=16, lat=us)
+    def pick(out, in_, pattern, base):
+        go = lambda: g.affine_select(ap(*out), ap(*in_), pattern, ALU.is_equal, 0.0, base, 1)
+        note({"G": (0.17 + 2 * width(out) * CY, go)}, [in_], [out])
 
-    def store(sem, out, src, us):
-        note("Y", 0.1, [(lambda: g.sync.dma_start(out, ap(*src)), True)], [src], [], sem=sem, val=16, lat=us)
+    def dma(q, sem, out, src, us):
+        eng = g.sync if q == "Y" else act
+        go = lambda: eng.dma_start(val(out), val(src))
+        note({q: (0.06, go)}, cols(src), cols(out), sem=sem, val=16, lat=us)
 
-    def gather(eng, out, win, lst, bias=None, outstep=1):
+    def gather(out, win, lst, bias=0.0, both=True):
         n = 16 * (lst[2] - lst[1])
         w = lambda: ap(*win).indirect(ap(*lst))
-        if eng == "S":
-            go = lambda: act.activation(ap(*out), w(), AF.Copy)
-        elif bias is None:
-            go = lambda: vec.tensor_copy(ap(out[0], out[1], out[2], outstep), w())
+        if bias:
+            alts = {"V": (VF + n * CY * GA, lambda: vec.tensor_scalar(ap(*out), w(), bias, None, ALU.add))}
         else:
-            go = lambda: vec.tensor_scalar(ap(*out), w(), bias, None, ALU.add)
-        note(eng, 0.07 + n * CY * GA, [(go, True)], [win, lst], [out])
+            alts = {"V": (VF + n * CY * GA, lambda: vec.tensor_copy(ap(*out), w()))}
+        if both:
+            alts["S"] = (SF + n * CY * GA, lambda: act.activation(ap(*out), w(), AF.Copy, bias=bias))
+        note(alts, [win, lst], [out])
 
     def scatter(win, lst, src):
         n = 16 * (lst[2] - lst[1])
-        note("V", 0.07 + n * CY * SC, [(lambda: vec.tensor_copy(ap(*win).indirect(ap(*lst)), ap(*src)), True)],
-             [lst, src], [win])
+        note({"V": (VF + n * CY * SC, lambda: vec.tensor_copy(ap(*win).indirect(ap(*lst)), ap(*src)))}, [lst, src], [win])
 
     def send(t, kind, src, w, dstname):
         dsts = [cores[target(rank, t, m, n_ranks)] for m in (1, 2, 3)]
@@ -194,307 +205,324 @@ def rank_program(g, core, T, topo):
                                             remote_sem=T.sem["%s%d" % (kind, t)],
                                             src=ap(src, w * m, w * m + w), dst=ap(dstname, w * (m - 1), w * m)))
             sent[0] += sum(len(e) for e in engs)
-            return g.remote_dma_fused(tr, local_sem=T.sem.loc)
-        i = note("G", 0.6, [(go, False)], [(src, w, 4 * w)], [])
+            g.remote_dma_fused(tr, local_sem=T.sem.loc)
+        i = note({"G": (0.5, go)}, [(src, w, 4 * w)], [])
         total = 0
         for m in (1, 2, 3):
             for s in range(n_ranks):
                 if target(s, t, m, n_ranks) == rank:
                     ds = [cores[target(s, t, x, n_ranks)] for x in (1, 2, 3)]
                     total += len(engine_split(topo, cores[s], ds)[m - 1])
-        note("N", NL * (3.0 if w > 8 else 2.2), [], [], [(dstname, 0, 3 * w)], sem="%s%d" % (kind, t), val=total, after=i)
+        note({"N": (2.6 if w > 8 else 1.9, None)}, [], [(dstname, 0, 3 * w)], sem="%s%d" % (kind, t), val=total, after=i)
 
-    def col(j):
-        return ("DC", j, j + 1)
+    def col(j, part=1):
+        return ("DC", j, j + 1, part) if part != 1 else ("DC", j, j + 1)
 
     def pf(j):
         return ("PF", j, j + 1)
 
-    def kf(j):
-        return ("KF", 128 * j, 128 * j + 128)
-
     def sq(name):
         return (name, 0, 128)
 
-    load("ldc", ("CBI", 0, 512), T.cb[:], 3.0)
-    load("ldw", ("WTI", 0, 1), T.wt[:], 3.0)
-    load("ldx", ("XT", 0, 4096), T.x[:], 7.0)
-    load("ldp0", ("PK", 0, 1024), T.pk[:, 0:1024], 9.0)
-    load("ldp1", ("PK", 1024, 2048), T.pk[:, 1024:2048], 11.0)
+    lo, hi = (0, 64), (64, 128)
 
-    iota(("IOP", 0, 1), [[0, 1]], 0, 1)
-    iota(("IOC", 0, 144), [[1, 144]], 0, 0)
-    iota(("SI", 0, 32), [[16, 32]], 8192, 1)
-    iota(("II", 0, 32), [[1, 4], [64, 8]], 0, 4)
+    dma("Y", "ldx", ("XT", 0, 4096), T.x[:], 5.5)
+    dma("S", "ldc", ("CBI", 0, 512), T.cb[:], 3.0)
+    dma("Y", "ldp0", ("PK", 0, 1024), T.pk[:, 0:1024], 7.5)
+    dma("Y", "ldp1", ("PK", 1024, 2048), T.pk[:, 1024:2048], 9.5)
+    dma("S", "ldw", ("WTI", 0, 1), T.wt[:], 3.0)
+
+    iota(("PI", 0, 1), [[0, 1]], 0, 1)
+    iota(("IOF", 0, 256), [[1, 256]], 0, 0)
+    iota(("C2", 0, 128), [[0, 2], [2, 64]], 0, 0)
+    iota(("QI", 0, 512), [[0, 64], [8, 8]], -27, 0)
     fill(sq("ONE"), 1.0)
     fill(sq("CC"), 18.0)
-    for j, mask in ((0, 127), (1, 15), (2, 112), (3, 56), (4, 7), (5, 64)):
-        ts(("PI", j, j + 1), ("IOP", 0, 1), mask, ALU.bitwise_and)
-    cp(("PF", 0, 6), ("PI", 0, 6))
-    cp(("IOF", 0, 144), ("IOC", 0, 144))
-    ts(("CI", 0, 144), ("IOC", 0, 144), -7, ALU.add)
-    ts(("CI", 144, 288), ("CI", 0, 144), 63, ALU.bitwise_and)
-    cm16, cd16 = ("CI", 288, 416), ("CI", 416, 544)
-    ts(cm16, sq("IOC"), 15, ALU.bitwise_and)
-    ts(cd16, sq("IOC"), 112, ALU.bitwise_and)
-    ts(col(0), pf(2), 0.5, ALU.mult)
-    ts(("QB", 0, 135), ("CI", 144, 279), col(0), ALU.is_equal)
-    ts(("RM", 0, 16), ("IOF", 0, 16), pf(1), ALU.is_equal)
+    fill(("CC", 0, 8, (0, 32)), 18.25)
+    for j, mask in enumerate((15, 112, 126, 1)):
+        ts(("PI", j + 1, j + 2), ("PI", 0, 1), mask, ALU.bitwise_and)
+    cp(("PF", 0, 5), ("PI", 0, 5))
+    p, zone, g16, even, odd = [pf(j) for j in range(5)]
+    ts(sq("IDB"), sq("IOF"), p, ALU.is_equal)
+    ts(("RM", 0, 16), ("IOF", 0, 16), zone, ALU.is_equal)
+    ts(col(3), g16, 0.0625, ALU.mult, 128.0, ALU.add)
+    ts(("QB", 0, 256), ("IOF", 0, 256), col(3), ALU.is_equal)
     for k in range(15):
-        kk = k if k < 7 else k - 7
-        sa(("DX", 128 * k, 128 * k + 128), ("QB", 7 - kk, 135 - kk), AF.Copy, scale=("RM", k, k + 1))
-    for m in range(4):
-        cp(("C0", 128 * m, 128 * m + 128), ("CBI", m, 512), step=4)
-    ts(sq("CI"), sq("IOC"), 7, ALU.bitwise_and)
-    ts(col(1), pf(0), 0.0, ALU.is_equal)
-    ts(kf(0), sq("CI"), 7.0, ALU.is_equal, col(1), ALU.mult)
-    ts(sq("CA"), kf(0), 18.0, ALU.add)
-    ts(col(2), pf(3), 2.0, ALU.mult)
-    ts(kf(1), cd16, col(2), ALU.is_equal)
-    ts(col(3), pf(5), 32.0, ALU.is_lt)
-    ts(col(4), col(3), 512.0, ALU.mult)
-    ts(col(5), col(3), 256.0, ALU.mult, -256.0, ALU.add)
-    ts(kf(2), cm16, col(4), ALU.mult, col(5), ALU.add)
-    tt(sq("ZB"), kf(1), kf(2), ALU.mult)
-    ts(("RM8", 0, 8), ("IOF", 0, 8), pf(4), ALU.is_equal)
-    ts(col(6), ("RM8", 7, 8), col(3), ALU.mult)
-    tt(kf(3), cm16, cm16, ALU.mult)
-    ts(kf(3), kf(3), -256.0, ALU.mult, 256.0, ALU.add)
-    ts(kf(3), kf(3), col(6), ALU.mult)
-    tt(sq("KB"), kf(3), kf(1), ALU.mult)
-    ts(col(12), ("RM8", 7, 8), -1.0, ALU.mult, 1.0, ALU.add)
-    ts(kf(4), sq("ZB"), col(12), ALU.mult)
-    tt(sq("KB"), sq("KB"), kf(4), ALU.add)
-    ts(("RMA", 0, 8), ("RM8", 0, 8), col(6), ALU.max)
-    for k in range(1, 16):
-        if k <= 7:
-            sa(("ZL", 128 * k, 128 * k + 128), sq("KB"), AF.Copy, scale=("RMA", k - 1, k))
-        else:
-            sa(("ZL", 128 * k, 128 * k + 128), sq("ZB"), AF.Copy, scale=("RM8", k - 8, k - 7))
-    tt(col(7), pf(1), pf(1), ALU.mult)
-    ts(col(8), col(7), -256.0, ALU.mult)
-    ts(col(9), pf(2), 15.0, ALU.add)
-    ts(col(16), pf(2), 0.0, ALU.mult, -256.0, ALU.add)
-    ts(("S1", 0, 143), ("IOF", 0, 143), col(9), ALU.is_equal)
-    ts(sq("IDB"), sq("IOF"), pf(0), ALU.is_equal)
-    sa(sq("RZ"), sq("IDB"), AF.Copy, scale=("RM", 0, 1))
-    ts(col(10), pf(4), 1.0, ALU.add)
-    ts(kf(5), cm16, col(10), ALU.is_equal)
-    ts(col(11), col(3), -65536.0, ALU.mult, 4096.0, ALU.add)
-    ts(col(11), col(11), col(12), ALU.mult)
-    ts(kf(5), kf(5), col(11), ALU.mult)
-    ts(col(13), col(3), 313088.0, ALU.mult, 256.0, ALU.add)
-    ts(col(13), col(13), ("RM8", 7, 8), ALU.mult)
-    ts(kf(5), kf(5), col(13), ALU.add)
-    ts(kf(6), cm16, 0.5, ALU.is_gt)
-    ts(kf(7), cm16, MINS + 0.5, ALU.is_lt)
-    tt(kf(7), kf(7), kf(6), ALU.mult)
-    tt(kf(7), kf(7), kf(1), ALU.mult)
-    tt(sq("GC"), kf(5), kf(7), ALU.mult)
-    ts(col(14), pf(0), 1.0, ALU.add)
-    ts(kf(8), sq("IOF"), col(14), ALU.is_equal)
-    tt(kf(8), sq("IDB"), kf(8), ALU.subtract)
-    tt(sq("DF"), kf(8), kf(6), ALU.mult)
-    ts(sq("BO"), cd16, pf(2), ALU.is_equal, 0.5, ALU.mult)
+        lin(("DX", 128 * k, 128 * k + 128), ("QB", 120 - 8 * k, 248 - 8 * k), ("RM", k, k + 1))
+    ts(col(4), p, 2.0, ALU.mult)
+    ts(("DU", 0, 128), sq("C2"), col(4), ALU.is_equal)
+    ts(("DU", 128, 256), sq("C2"), 128.0, ALU.add, col(4), ALU.is_equal)
+    for m in ORDER:
+        cp(("C0", 128 * m, 128 * m + 128), ("CBI", m, 512, 4))
+    fill(col(0, lo), -1792.0)
+    fill(col(0, hi), -2048.0)
+    fill(col(1, lo), 1.0)
+    fill(col(1, hi), -1.0)
+    ts(("MK", 0, 512), ("QI", 0, 512), col(1), ALU.mult, -2.0, ALU.add)
+    for half in (lo, hi):
+        pick(("MK", 0, 512, half), ("MK", 0, 512, half), [[-8, 8], [-1, 8], [0, 8]], 0)
+    lin(("D0", 0, 512), ("QI", 0, 512), 2.0 ** 18, -2.0 ** 20 - 512)
+    ts(col(2), odd, 511.0, ALU.mult, 1.0, ALU.add)
+    ts(("PR", 0, 64), ("C2", 0, 64), even, ALU.is_equal, col(2), ALU.mult)
+    for b in range(2):
+        fill(("SO", 1024 * b, 1024 * b + 64), 51.75 * 2 ** 18 - 3584)
+    ts(sq("I32"), sq("IOF"), p, ALU.is_equal)
+    ts(sq("RZ"), sq("IOF"), 16.0, ALU.mult, p, ALU.is_equal)
+    ts(col(5), p, 7.5, ALU.is_gt, -256.0, ALU.mult)
+    fill(col(6), 0.0)
+    fill(col(6, (0, 2)), 608.0)
+    fill(col(6, (0, 1)), -199.0 * 2 ** 13)
+    ts(sq("NZ"), sq("IDB"), col(5), ALU.mult, col(6), ALU.add)
+    lin(sq("NR"), sq("IDB"), -512.0)
+    pick(sq("PM"), sq("ONE"), [[-1, 8], [-8, 16]], 0)
+    pick(sq("PS"), sq("ONE"), [[-1, 8], [-8, 16]], 8)
+    tt(sq("DF"), sq("PM"), sq("PS"), ALU.subtract)
+    fill(("DF", 0, 128, 16), 0.0)
+    iota(sq("GI"), [[16, 8], [0, 16]], 0, 0)
+    ts(sq("BO"), sq("GI"), g16, ALU.is_equal, 0.5, ALU.mult)
+    ts(("S1", 0, 143), ("IOF", 0, 143), -15.0, ALU.add, g16, ALU.is_equal)
     cp(("WTF", 0, 1), ("WTI", 0, 1))
-    sa(("LW", 0, 143), ("S1", 0, 143), AF.Copy, scale=("WTF", 0, 1))
-    ts(col(15), pf(2), 4.0, ALU.mult)
-    ts(("II", 0, 32), ("II", 0, 32), col(15), ALU.subtract)
-    ts(("SI", 0, 32), ("SI", 0, 32), pf(2), ALU.subtract)
+    lin(("LW", 0, 143), ("S1", 0, 143), ("WTF", 0, 1))
+    iota(("SI", 0, 32), [[16, 32]], 8192, 1)
+    iota(("II", 0, 32), [[1, 4], [64, 8]], 0, 4)
+    ts(col(10), g16, 4.0, ALU.mult)
+    ts(("II", 0, 32), ("II", 0, 32), col(10), ALU.subtract)
+    ts(("SI", 0, 32), ("SI", 0, 32), g16, ALU.subtract)
+    cur[0] = "u"
     for c in (0, 1024):
         ts(("BT", 512 + c, 1536 + c), ("PK", c, c + 1024), 4095, ALU.bitwise_and)
         ts(("BT", 2560 + c, 3584 + c), ("PK", c, c + 1024), 12, ALU.logical_shift_right)
-    for k in range(16):
-        sa(("DB", 128 * k, 128 * k + 128), sq("IDB"), AF.Copy, scale=("RM", k, k + 1))
-    cp(sq("I16"), sq("IDB"))
-    sa(sq("PP"), sq("IDB"), AF.Copy, scale=2048.0)
-    sa(sq("PN"), sq("IDB"), AF.Copy, scale=-2048.0)
+    cur[0] = "c"
+    fill(("DB", 0, 2048), 1.0)
+    pick(("DB", 0, 2048), ("DB", 0, 2048), [[255, 16], [-16, 8], [-256, 16]], 0)
+    lin(sq("PP"), sq("IDB"), 2048.0)
+    lin(sq("PN"), sq("IDB"), -2048.0)
 
     for t in range(NR):
         C, V, OF, NX = "C%d" % t, "V%d" % t, "OF%d" % t, "NX%d" % t
-        cur[0] = "c"
+        Y = lambda i, a=0, b=32: ("YW", 32 * i + a, 32 * i + b)
+
+        def wrapped(a, b):
+            for c, mat, src in ((0, "LW", V), (32, "S1", "SG")):
+                mms([(("x0", c + a, c + b), (mat, 15 - r, 143 - r), (src, 16 * a + r, 16 * b, 16)) for r in range(16)])
+            ts(Y(2, a, b), ("x0", 32 + a, 32 + b), -3.0, ALU.is_gt, 4096.0, ALU.mult)
+            tt(Y(3, a, b), Y(2, a, b), ("II", a, b), ALU.add)
+
+        def places(a, b):
+            ts(Y(0, a, b), ("x0", a, b), acol, ALU.add, 512.0, ALU.mult)
+            ts(Y(1, a, b), Y(0, a, b), 3584, ALU.bitwise_and)
+            tt(Y(4, a, b), Y(1, a, b), Y(3, a, b), ALU.add)
+            cp((OF, a, b), Y(4, a, b))
+
+        cur[0] = "cin"
         send(t, "cin", C, 128, "CIN%d" % t)
         for q in range(4):
             m = ORDER[q]
-            s0, j0, z0, r0 = 128 * m, 2048 * m, 256 * q, 2048 * q
-            for h in range(2):
-                cur[0] = "x%d%d" % (q, h)
-                gather("V" if (q, h) in XV else "S", ("G", j0 + 1024 * h, j0 + 1024 * h + 1024), ("XT", 0, 4096),
-                       (C, s0 + 64 * h, s0 + 64 * h + 64))
-            E, VB = BANKS[q % 2], BANKS[6 + q % 2]
-            cur[0] = "e%d" % q
-            it = [(A(E, 0, 128), A("CA", 0, 128), A("ONE", 0, 128), True, False, 128)]
-            for k in range(15):
-                if k == 7:
-                    it.append((A(E, 128, 256), A("CC", 0, 128), A("ONE", 0, 128), True, False, 128))
-                o = A(E, 0, 128) if k < 7 else A(E, 128, 256)
-                it.append((o, A("DX", 128 * k, 128 * k + 128), A("G", j0 + k, j0 + 2048, 16), False, k in (6, 14), 128))
-            mms(it, [sq("CA"), sq("CC"), sq("ONE"), ("DX", 0, 1920), ("G", j0, j0 + 2048)], [(E, 0, 256)])
+            s0, j0, z0, o0 = 128 * m, 2048 * m, 256 * q, 1024 * (q % 2)
+            X, D = BANKS[q % 2], BANKS[2 + 2 * (q % 3):4 + 2 * (q % 3)]
+            for c in range(0, 128, ECH):
+                cur[0] = "x%d" % q
+                for a in range(s0 + c, s0 + c + ECH, XCH):
+                    gather(("G", 16 * a, 16 * (a + XCH)), ("XT", 0, 4096), (C, a, a + XCH))
+                cur[0] = "e%d" % q
+                ja, jb = j0 + 16 * c, j0 + 16 * (c + ECH)
+                mms([((X, c, c + ECH), sq("CC"), ("ONE", 0, ECH))] +
+                    [((X, c, c + ECH), ("DX", 128 * k, 128 * k + 128), ("G", ja + k, jb, 16)) for k in range(15)])
             cur[0] = "t%d" % q
-            th, zz = ("TH", z0, z0 + 256), ("Z", z0, z0 + 256)
-            if q in THS:
-                sa(th, (E, 0, 256), AF.Copy, bias=-7.5)
-            else:
-                ts(th, (E, 0, 256), -7.5, ALU.add)
-            tt(zz, (E, 0, 256), th, ALU.subtract)
-            sa(zz + (64, 128), zz + (64, 128), AF.Square)
-            for b, ks in enumerate(SLOTS):
-                D = BANKS[2 + b]
-                za = z0 if b < 2 else z0 + 128
-                it, rd = [], [("ZL", 128 * ks[0], 128 * ks[-1] + 128), ("Z", za, za + 128)]
-                for x, k in enumerate(ks):
-                    o = A(D, 128 * x, 128 * x + 128)
-                    it.append((o, A("ZL", 128 * k, 128 * k + 128), A("Z", za, za + 128), True, k <= MINS, 128))
-                    if k > MINS:
-                        it.append((o, A("IDB", 0, 128), A("G", j0 + k, j0 + 2048, 16), False, True, 128))
-                if ks[-1] > MINS:
-                    rd += [sq("IDB"), ("G", j0, j0 + 2048)]
-                n = 128 * len(ks)
-                cur[0] = "d%d%d" % (q, b)
-                mms(it, rd, [(D, 0, n)])
-                rb = r0 + 128 * (ks[0] - 1)
-                cur[0] = "r%d%d" % (q, b)
-                if ks[-1] > MINS:
-                    sa(("R", rb, rb + n), (D, 0, n), AF.Relu, bias=col(16) if b < 2 else col(8))
-                else:
-                    for x, k in enumerate(ks):
-                        tt(("R", rb + 128 * x, rb + 128 * x + 128), (D, 128 * x, 128 * x + 128),
-                           ("G", j0 + k, j0 + 2048), ALU.min, step1=16)
-            for b, ks in enumerate(SLOTS):
-                it, rd = [], [("S1", 0, 143), ("R", r0 + 128 * (ks[0] - 1), r0 + 128 * ks[-1])]
-                if b == 0:
-                    it.append((A(VB, 0, 128), A("RZ", 0, 128), A("G", j0, j0 + 2048, 16), True, False, 128))
-                    it.append((A(VB, 0, 128), A("GC", 0, 128), A("Z", z0, z0 + 128), False, False, 128))
-                    rd += [sq("RZ"), sq("GC"), ("G", j0, j0 + 2048), ("Z", z0, z0 + 128)]
-                for k in ks:
-                    rb = r0 + 128 * (k - 1)
-                    it.append((A(VB, 0, 128), A("S1", 15 - k, 143 - k), A("R", rb, rb + 128), False, k == 15, 128))
-                cur[0] = "s%d%d" % (q, b)
-                mms(it, rd, [(VB, 0, 128)])
+            th, z = ("TH", s0, s0 + 128), ("Z", s0, s0 + 128)
+            lin(th, sq(X), 1.0, -7.5)
+            tt(z, sq(X), th, ALU.subtract)
+            mms([((X, 128 + 128 * b, 256 + 128 * b), ("DU", 128 * b, 128 * b + 128), z) for b in range(2)], groups=1)
+            sa(("U", z0, z0 + 256), (X, 128, 384), AF.Square, scale=256.0, bias=col(0))
+            for b in range(2):
+                c = 64 * (1 - b)
+                cur[0] = "p%d" % q
+                mms([((D[b], 64 * kk, 64 * kk + 64), ("G", j0 + 8 * b + kk, j0 + 2048, 16), ("PR", 0, 64))
+                     for kk in range(1 - b, 8)], last=False)
+                cur[0] = "d%d" % q
+                mms([((D[b], c, 512), ("U", z0 + 128 * b, z0 + 128 * b + 128), ("MK", c, 512))], first=False)
+                cur[0] = "s%d" % q
+                scan(("SO", o0 + 512 * b + c, o0 + 512 * b + 512), ("D0", c, 512), (D[b], c, 512))
             cur[0] = "v%d" % q
-            vq = (V, s0, s0 + 128)
-            sa(vq, (VB, 0, 128), AF.Copy)
-            mms([(A(VB, 128, 256), A("DF", 0, 128), A(*vq), True, True, 128)], [sq("DF"), vq], [(VB, 128, 256)])
-            sa(("AB", s0, s0 + 128), (VB, 128, 256), AF.Abs)
+            so, rr, vp, vq = ("SO", o0 + 7, o0 + 1024, 8), ("RR", s0, s0 + 128), ("VP", s0, s0 + 128), (V, s0, s0 + 128)
+            mms([(sq(D[0]), sq("NZ"), z), (sq(D[0]), so, sq("I32"))])
+            mms([(sq(D[1]), sq("NZ"), z), (sq(D[1]), sq("RZ"), ("G", j0, j0 + 2048, 16)), (sq(D[1]), so, sq("I32"))], last=False)
+            lin(rr, sq(D[0]), 2.0 ** -9, -2.5 + 2.0 ** -10)
+            mms([(sq(D[1]), sq("NR"), rr)], first=False)
+            tt(vp, sq(D[1]), rr, ALU.max)
+            mms([((D[0], 128, 256), sq("DF"), vp)])
+            mms([((D[1], 128, 256), sq("PM"), vp)])
+            sa(("AB", s0, s0 + 128), (D[0], 128, 256), AF.Abs)
             sa(("SG", s0, s0 + 128), ("AB", s0, s0 + 128), AF.Sign, bias=-64.5, acc=("ACC", q, q + 1))
+            lin(vq, (D[1], 128, 256), 1.0, -1280.0)
             if q == 2:
+                cur[0] = "vin"
                 send(t, "vin", V, 128, "VIN%d" % t)
+                cur[0] = "h"
+                ts(("ACC", 4, 5), ("ACC", 0, 1), ("ACC", 1, 2), ALU.add, ("ACC", 2, 3), ALU.add)
+                wrapped(8, 32)
         cur[0] = "a"
-        for qs in ((0, 1, 2), (3,)):
-            mms([(A("e0", 0, 1), A("BO", 0, 128), A("ACC", q, q + 1), q == 0, q == 3, 256) for q in qs],
-                [sq("BO"), ("ACC", qs[0], qs[-1] + 1)], [("e0", 0, 1)])
-        for bank, mat, src in (("e1", "LW", V), ("d2", "S1", "SG")):
-            mms([(A(bank, 0, 32), A(mat, 15 - r, 143 - r), A(src, r, 512, 16), r == 0, r == 15, 32) for r in range(16)],
-                [(mat, 0, 143), (src, 0, 512)], [(bank, 0, 32)])
-        Y = [("YW", 32 * i, 32 * i + 32) for i in range(10)]
-        acol, hw, nw = ("e0", 0, 1), ("e1", 0, 32), ("d2", 0, 32)
-        ts(Y[0], hw, acol, ALU.add, 512.0, ALU.mult)
-        ts(Y[1], Y[0], 3584, ALU.bitwise_and)
-        ts(Y[2], nw, -3.0, ALU.is_gt, 4096.0, ALU.mult)
-        tt(Y[3], Y[2], ("II", 0, 32), ALU.add)
-        tt(Y[4], Y[1], Y[3], ALU.add)
-        cp((OF, 0, 32), Y[4])
+        acol = ("x1", 0, 1)
+        mms([(acol, sq("BO"), ("ACC", q, q + 1)) for q in (4, 3)])
+        places(8, 32)
         send(t, "oin", OF, 8, "OIN%d" % t)
         cur[0] = "n"
-        ts(Y[5], hw, 37.0, ALU.mult, acol, ALU.add)
-        ts(Y[6], Y[5], 4095, ALU.bitwise_and)
-        ts(Y[7], nw, -3.0, ALU.is_lt, 8704.0, ALU.mult)
-        tt(Y[8], Y[6], Y[7], ALU.add)
-        tt(Y[9], Y[8], ("SI", 0, 32), ALU.max)
-        ts((NX, 0, 32), Y[9], -8192.0, ALU.add)
-        for c in range(0, 512, BCH):
-            cur[0] = "b%d" % (c // 64)
-            gather("V", ("GB", 16 * c, 16 * (c + BCH)), ("BT", 512, 4608), (C, c, c + BCH), bias=-2048.0)
+        wrapped(0, 8)
+        places(0, 8)
+        ts(Y(5), ("x0", 0, 32), 37.0, ALU.mult, acol, ALU.add)
+        ts(Y(7), ("x0", 32, 64), -3.0, ALU.is_lt, 8704.0, ALU.mult)
+        ts(Y(6), Y(5), 4095, ALU.bitwise_and)
+        tt(Y(8), Y(6), Y(7), ALU.add)
+        tt(Y(9), Y(8), ("SI", 0, 32), ALU.max)
+        ts((NX, 0, 32), Y(9), -8192.0, ALU.add)
         cur[0] = "m"
         ts(("CF", 0, 512), (C, 0, 512), -2048.0, ALU.add)
-        for m in ORDER:
-            a, b = 128 * m, 128 * m + 128
-            it = [(A("d0", a, b), A("DB", 128 * k, 128 * k + 128), A("GB", 2048 * m + k, 2048 * m + 2048, 16), k == 0, False, 128)
-                  for k in range(16)]
-            it.append((A("d0", a, b), A("PP", 0, 128), A("SG", a, b), False, True, 128))
-            mms(it, [("DB", 0, 2048), ("GB", 2048 * m, 2048 * m + 2048), sq("PP"), ("SG", a, b)], [("d0", a, b)])
-        mms([(A("d1", 0, 512), A("I16", 0, 128), A("CF", 0, 512), True, False, 512),
-             (A("d1", 0, 512), A("PN", 0, 128), A("SG", 0, 512), False, True, 512)],
-            [sq("I16"), ("CF", 0, 512), sq("PN"), ("SG", 0, 512)], [("d1", 0, 512)])
-        sa(("X2S", 0, 512), ("d1", 0, 512), AF.Copy)
-        tt(("BT", 0, 512), ("d0", 0, 512), ("X2S", 0, 512), ALU.max)
+        mms([(("d4", 0, 512), sq("IDB"), ("CF", 0, 512)), (("d4", 0, 512), sq("PN"), ("SG", 0, 512))])
+        lin(("X2S", 0, 512), ("d4", 0, 512), 1.0)
+        for q in range(4):
+            M = BANKS[4 + q % 2]
+            for a in range(128 * ORDER[q], 128 * ORDER[q] + 128, ECH):
+                b = a + ECH
+                cur[0] = "b%d" % q
+                for c in range(a, b, BCH):
+                    gather(("GB", 16 * c, 16 * (c + BCH)), ("BT", 512, 4608), (C, c, c + BCH), bias=-2048.0)
+                cur[0] = "m%d" % q
+                mms([((M, a, b), ("DB", 128 * k, 128 * k + 128), ("GB", 16 * a + k, 16 * b, 16)) for k in range(1, 16)]
+                    + [((M, a, b), sq("PP"), ("SG", a, b))])
+            tt(("BT", b - 128, b), (M, b - 128, b), ("X2S", b - 128, b), ALU.max)
         cur[0] = "o"
-        scatter(("BT", 512, 8704), (OF, 0, 8), (C, 0, 128))
         scatter(("XT", 0, 8192), (OF, 0, 8), (V, 0, 128))
+        scatter(("BT", 512, 8704), (OF, 0, 8), (C, 0, 128))
         cur[0] = "z"
         scatter(("BT", 512, 8704), ("OIN%d" % t, 0, 24), ("CIN%d" % t, 0, 384))
         scatter(("XT", 0, 8192), ("OIN%d" % t, 0, 24), ("VIN%d" % t, 0, 384))
         for m in ORDER:
-            if t + 1 < NR:
-                gather("V", ("C%d" % (t + 1), 128 * m, 128 * m + 128), ("BT", 0, 4608), (NX, 8 * m, 8 * m + 8))
-            else:
-                gather("V", ("YC", m, 512), ("BT", 0, 4608), (NX, 8 * m, 8 * m + 8), outstep=4)
+            out = ("C%d" % (t + 1), 128 * m, 128 * m + 128) if t + 1 < NR else ("YC", m, 512, 4)
+            gather(out, ("BT", 0, 4608), (NX, 8 * m, 8 * m + 8), both=False)
 
-    store("stx", T.yx[:], ("XT", 0, 4096), 7.0)
-    store("stc", T.yc[:], ("YC", 0, 512), 3.0)
-    if CAP is not None:
-        CAP.append(ops)
-        return
+    cur[0] = "st"
+    dma("Y", "stx", T.yx[:], ("XT", 0, 4096), 5.5)
+    dma("Y", "stc", T.yc[:], ("YC", 0, 512), 3.0)
     run_queues(g, T, ops, sent)
 
 
-def run_queues(g, T, ops, sent):
+def schedule(ops):
     n = len(ops)
     users = [[] for _ in range(n)]
     for i, o in enumerate(ops):
         for j in o["deps"]:
             users[j].append(i)
-    wake = 0.12
     prio = [0.0] * n
     for i in range(n - 1, -1, -1):
-        prio[i] = ops[i]["dur"] + ops[i]["lat"] + max([prio[u] + wake for u in users[i]] or [0.0])
+        prio[i] = min(d for d, _ in ops[i]["alts"].values()) + ops[i]["lat"] + max([prio[u] + WAKE for u in users[i]] or [0.0])
     prio = [p + BON.get(o["tag"], 0.0) for p, o in zip(prio, ops)]
     left = [len(o["deps"]) for o in ops]
     ready = [0.0] * n
-    free, cand = {}, {}
-    for i, o in enumerate(ops):
-        free[o["q"]] = 0.0
-        cand.setdefault(o["q"], [])
-        if left[i] == 0:
-            cand[o["q"]].append(i)
+    free = {q: 0.0 for o in ops for q in o["alts"]}
+    cand = [i for i in range(n) if left[i] == 0]
     seq = []
-    while len(seq) < n:
-        best = None
-        for q in sorted(cand):
-            if cand[q]:
-                s = min(max(ready[i], free[q]) for i in cand[q])
-                if best is None or s < best[0]:
-                    best = (s, q)
-        s, q = best
-        pick = max((i for i in cand[q] if max(ready[i], free[q]) <= s + LOOK), key=lambda i: (prio[i], -i))
+    while cand:
+        s, q = min((max(ready[i], free[q]), q) for i in cand for q in ops[i]["alts"])
+        pick = max((i for i in cand if q in ops[i]["alts"] and max(ready[i], free[q]) <= s + LOOK),
+                   key=lambda i: (prio[i], -i))
         o = ops[pick]
+        dur = o["alts"][q][0]
         st = max(ready[pick], free[q])
         if q != "N":
-            free[q] = st + o["dur"]
-        end = st + o["dur"] + o["lat"]
-        cand[q].remove(pick)
-        seq.append(pick)
+            free[q] = st + dur
+        cand.remove(pick)
+        seq.append((pick, q))
         for u in users[pick]:
-            gap = wake
-            if ops[u]["q"] == q:
-                gap = 0.06 if ops[u]["deps"][pick] else 0.0
-            ready[u] = max(ready[u], end + gap)
+            ready[u] = max(ready[u], st + dur + (o["lat"] + WAKE if ops[u]["deps"][pick] else 0.0))
             left[u] -= 1
             if left[u] == 0:
-                cand[ops[u]["q"]].append(u)
+                cand.append(u)
+    return seq
 
+
+def improve(ops, seq):
+    n = len(ops)
+    order, qof = [i for i, q in seq], [None] * n
+    for i, q in seq:
+        qof[i] = q
+    users = [set() for _ in range(n)]
+    above = [set() for _ in range(n)]
+    hard = [[] for _ in range(n)]
+    for i, o in enumerate(ops):
+        for j in sorted(o["deps"], reverse=True):
+            users[j].add(i)
+            if o["deps"][j] and j not in above[i]:
+                hard[i].append(j)
+                above[i] |= above[j] | {j}
+    dur = [{q: d for q, (d, _) in o["alts"].items()} for o in ops]
+    lat = [o["lat"] for o in ops]
+    start, why = [0.0] * n, [-1] * n
+
+    def clock():
+        end, free, last = [0.0] * n, dict.fromkeys("GNPSVY", 0.0), dict.fromkeys("GNPSVY", -1)
+        for i in order:
+            q = qof[i]
+            st, w = free[q], last[q]
+            for j in hard[i]:
+                e = end[j] + (SAME if qof[j] == q else WAKE)
+                if e > st:
+                    st, w = e, j
+            start[i], why[i] = st, w
+            st += dur[i][q]
+            if q != "N":
+                free[q], last[q] = st, i
+            end[i] = st + lat[i]
+        return max(end), end
+
+    rnd = np.random.RandomState(SEED).random_sample((MOVES, 6)).tolist()
+    now = clock()[0]
+    best = (now, list(order), list(qof))
+    for it, (r0, r1, r2, r3, r4, r5) in enumerate(rnd):
+        if it % 50 == 0:
+            total, end = clock()
+            path = [end.index(total)]
+            while why[path[-1]] >= 0:
+                path.append(why[path[-1]])
+            order.sort(key=lambda i: start[i])
+        p = order.index(path[int(r1 * len(path))]) if r0 < 0.6 else int(r1 * n)
+        if r0 < 0.3:
+            p = min(n - 1, max(0, p + int(r0 * 80) - 12))
+        i, span = order[p], (4, 10, 25, 60)[int(r2 * 4)]
+        was = qof[i]
+        if len(dur[i]) > 1 and r3 < 0.4:
+            qof[i] = "S" if was == "V" else "V"
+        a = b = p
+        while a > 0 and p - a < span and order[a - 1] not in ops[i]["deps"]:
+            a -= 1
+        while b < n - 1 and b - p < span and order[b + 1] not in users[i]:
+            b += 1
+        to = a + int(r4 * (b - a + 1))
+        order.insert(to, order.pop(p))
+        total = clock()[0]
+        if total <= now - (HEAT * (1 - it / MOVES) + 0.003) * math.log(r5 + 1e-12):
+            now = total
+            if now < best[0]:
+                best = (now, list(order), list(qof))
+        else:
+            order.insert(p, order.pop(to))
+            qof[i] = was
+    return [(i, best[2][i]) for i in best[1]]
+
+
+def run_queues(g, T, ops, sent):
     eng = {"V": g.vector, "S": g.scalar, "P": g.tensor, "G": g, "Y": g.sync}
     cnt = {"V": 0, "S": 0, "P": 0, "G": 0}
-    clock = {q: {} for q in free}
+    clock = {q: {} for q in eng}
     know, done = {}, {}
-    for i in seq:
+    if not PLAN:
+        PLAN.extend(improve(ops, schedule(ops)))
+    for i, q in PLAN:
         o = ops[i]
-        q = o["q"]
-        ck = clock[q]
         if q == "N":
             know[i] = {o["sem"]: o["val"]}
             done[i] = (o["sem"], o["val"])
             continue
+        ck = clock[q]
         need = {}
         for j, hard in o["deps"].items():
             if hard:
@@ -507,13 +535,15 @@ def run_queues(g, T, ops, sent):
             eng[q].wait_ge(T.sem[sem], val)
             for s2, v2 in know[j].items():
                 ck[s2] = max(ck.get(s2, 0), v2)
-        for th, inc in o["th"]:
-            ins = th()
-            if inc and o["sem"]:
-                ins.then_inc(T.sem[o["sem"]], 16)
-            elif inc:
-                cnt[q] += 1
-                ins.then_inc(T.sem["q" + q], 1)
+        if q == "G" and ck.get("qG", 0) < cnt[q]:
+            g.wait_ge(T.sem.qG, cnt[q])
+            ck["qG"] = cnt[q]
+        ins = o["alts"][q][1]()
+        if o["sem"]:
+            ins.then_inc(T.sem[o["sem"]], 16)
+        elif ins is not None:
+            cnt[q] += 1
+            ins.then_inc(T.sem["q" + q], 1)
         know[i] = dict(ck)
         done[i] = (o["sem"], o["val"]) if o["sem"] else ("q" + q, cnt.get(q, 0))
         know[i][done[i][0]] = done[i][1]

@@ -5,25 +5,27 @@ from concourse.mybir import AluOpType as ALU, ActivationFunctionType as AF
 
 NR = 3
 ORDER = [1, 2, 3, 0]
-XCH = 32
+XCH = (64, 64, 64, 64)
+BCH = (32, 32, 64, 64)
 ECH = 64
-BCH = 32
+LAST = 51.75 * 2 ** 18 - 3570
 LOOK = 0.15
-BON = {}
-CY, GA, SC, TE, VF, SF, WAKE, SAME = 0.00083, 1.5, 3.6, 0.00045, 0.06, 0.075, 0.13, 0.06
-MOVES, HEAT, SEED = 100000, 0.08, 0
+BON = {"u": 6.0}
+CY, GA, SC, TE, VF, SF, WAKE, NEAR = 0.00083, 1.56, 3.8, 0.00043, 0.055, 0.07, 0.12, 0.06
+RATES = (1.0,)
+MOVES, HEAT, TWINS, SEED = 240000, 0.15, 0.85, 1
 PLAN = []
 
 SCRATCH = {}
 for _spec in (
-        "XT 8192 bfloat16, BT 8704 int32, PK 2048 int32, CBI 512 int32, WTI 1 int32, WTF 1 float32, G 8192 bfloat16, "
+        "XT 12288 bfloat16, BT 12800 int32, PK 2048 int32, CBI 512 int32, WTI 1 int32, WTF 1 float32, G 8192 bfloat16, "
         "GB 8192 float16, CF 512 float16, TH 512 bfloat16, Z 512 bfloat16, U 1024 bfloat16, SO 2048 float32, "
         "RR 512 float16, VP 512 float16, AB 512 bfloat16, SG 512 bfloat16, ACC 8 float32, X2S 512 float32, YW 320 int32, "
-        "YC 512 float32, SI 32 int32, II 32 int32, PI 8 int32, PF 8 float32, DC 24 float32, IOF 256 float32, "
-        "C2 128 float32, QI 512 bfloat16, D0 512 float32, MK 512 bfloat16, GI 128 float32, RM 16 float32, "
-        "S1 144 bfloat16, LW 144 bfloat16, QB 256 bfloat16, RZ 128 bfloat16, IDB 128 bfloat16, I32 128 float32, "
-        "DX 1920 bfloat16, PR 64 bfloat16, DU 256 bfloat16, NZ 128 bfloat16, NR 128 bfloat16, "
-        "PM 128 bfloat16, PS 128 bfloat16, DF 128 bfloat16, BO 128 float32, CC 128 bfloat16, ONE 256 bfloat16, "
+        "YC 512 float32, SI 32 int32, II 32 int32, PI 8 int32, PF 8 float32, DC 24 float32, IOF 144 float32, "
+        "C2 128 float32, QI 512 bfloat16, D0 512 float32, MK 512 bfloat16, GI 128 float32, "
+        "S1 144 bfloat16, LW 144 bfloat16, RZ 128 bfloat16, IDB 128 bfloat16, I32 128 float32, "
+        "PR 64 bfloat16, NZ 128 bfloat16, NR 128 bfloat16, "
+        "PM 128 bfloat16, PS 128 bfloat16, DF 128 bfloat16, BO 128 float32, CC 128 bfloat16, ONE 128 bfloat16, "
         "DB 2048 bfloat16, PP 128 bfloat16, PN 128 bfloat16").split(", ") + [
         "%s%d %s" % (n, t, d) for t in range(NR) for n, d in (
             ("C", "512 uint16"), ("V", "512 bfloat16"), ("OF", "32 uint16"), ("NX", "32 uint16"),
@@ -44,14 +46,16 @@ def shares(pool, n):
 
 
 def engine_split(topo, src, dsts):
-    lists = [topo.engines(src, d) for d in dsts]
-    pool = min(lists, key=len)
-    narrow = [i for i in range(len(dsts)) if len(lists[i]) == len(pool)]
-    wide = [i for i in range(len(dsts)) if len(lists[i]) > len(pool)]
+    lists = {m: topo.engines(src, d) for m, d in dsts.items()}
+    pool = min(lists.values(), key=len)
+    narrow = [m for m in dsts if len(lists[m]) == len(pool)]
+    wide = [m for m in dsts if len(lists[m]) > len(pool)]
+    if len(narrow) == 3 and topo.chip(dsts[narrow[0]]) != topo.chip(src):
+        return [dict(zip(narrow, shares(pool, 2))), {narrow[2]: pool}]
     got = dict(zip(narrow, shares(pool, len(narrow))))
     if wide:
         got.update(zip(wide, shares([e for e in lists[wide[0]] if e not in pool], len(wide))))
-    return [got[i] for i in range(len(dsts))]
+    return [got]
 
 
 def target(r, t, m, n):
@@ -64,10 +68,10 @@ def rank_program(g, core, T, topo):
         return
     cores = list(T.cores)
     n_ranks = len(cores)
-    ops, hist, sent, cur = [], {}, [0], ["c"]
+    ops, hist, sent, cur, landing = [], {}, [0], ["c"], {}
     vec, act, ten = g.vector, g.scalar, g.tensor
 
-    def note(alts, rd, wr, sem=None, val=0, after=None, lat=0.0):
+    def note(alts, rd, wr, sem=None, val=0, after=(), lat=0.0, ind=0.0):
         idx = len(ops)
         pe = "P" in alts
         deps = {}
@@ -90,9 +94,8 @@ def rank_program(g, core, T, topo):
                     keep.append(e)
                 keep.append((idx, w, c0, c1))
                 hist[b] = keep
-        if after is not None:
-            deps[after] = True
-        ops.append({"alts": alts, "deps": deps, "sem": sem, "val": val, "lat": lat, "tag": cur[0]})
+        deps.update(dict.fromkeys(after, True))
+        ops.append({"alts": alts, "deps": deps, "sem": sem, "val": val, "lat": lat, "ind": ind, "tag": cur[0]})
         return idx
 
     def ap(b, c0, c1, x=1):
@@ -172,48 +175,43 @@ def rank_program(g, core, T, topo):
         go = lambda: g.affine_select(ap(*out), ap(*in_), pattern, ALU.is_equal, 0.0, base, 1)
         note({"G": (0.17 + 2 * width(out) * CY, go)}, [in_], [out])
 
-    def dma(q, sem, out, src, us):
+    def dma(q, sem, out, src, us, after=()):
         eng = g.sync if q == "Y" else act
         go = lambda: eng.dma_start(val(out), val(src))
-        note({q: (0.06, go)}, cols(src), cols(out), sem=sem, val=16, lat=us)
+        return note({q: (0.06, go)}, cols(src), cols(out), sem=sem, val=16, lat=us, after=after)
 
-    def gather(out, win, lst, bias=0.0, both=True):
+    def gather(out, win, lst, bias=0.0):
         n = 16 * (lst[2] - lst[1])
         w = lambda: ap(*win).indirect(ap(*lst))
-        if bias:
-            alts = {"V": (VF + n * CY * GA, lambda: vec.tensor_scalar(ap(*out), w(), bias, None, ALU.add))}
-        else:
-            alts = {"V": (VF + n * CY * GA, lambda: vec.tensor_copy(ap(*out), w()))}
-        if both:
-            alts["S"] = (SF + n * CY * GA, lambda: act.activation(ap(*out), w(), AF.Copy, bias=bias))
-        note(alts, [win, lst], [out])
+        on_v = lambda: vec.tensor_scalar(ap(*out), w(), bias, None, ALU.add) if bias else vec.tensor_copy(ap(*out), w())
+        on_s = lambda: act.activation(ap(*out), w(), AF.Copy, bias=bias)
+        note({"V": (VF + n * CY * GA, on_v), "S": (SF + n * CY * GA, on_s)}, [win, lst], [out], ind=n * CY * GA)
 
     def scatter(win, lst, src):
         n = 16 * (lst[2] - lst[1])
-        note({"V": (VF + n * CY * SC, lambda: vec.tensor_copy(ap(*win).indirect(ap(*lst)), ap(*src)))}, [lst, src], [win])
+        go = lambda: vec.tensor_copy(ap(*win).indirect(ap(*lst)), ap(*src))
+        note({"V": (VF + n * CY * SC, go)}, [lst, src], [win], ind=n * CY * SC)
 
-    def send(t, kind, src, w, dstname):
-        dsts = [cores[target(rank, t, m, n_ranks)] for m in (1, 2, 3)]
-        engs = engine_split(topo, core, dsts)
+    def send(t, kind, src, w, dstname, ms=(1, 2, 3)):
+        def calls(r):
+            return engine_split(topo, cores[r], {m: cores[target(r, t, m, n_ranks)] for m in ms})
 
         def go():
-            tr = []
-            for m in (1, 2, 3):
-                rid, pid = topo.addr(dsts[m - 1])[:2]
-                mask = sum(1 << e for e in engs[m - 1])
-                tr.append(RemoteDMATransfer(dst_ids=[DstId(rid=rid, pnc=pid)], dma_engine_mask=mask,
-                                            remote_sem=T.sem["%s%d" % (kind, t)],
-                                            src=ap(src, w * m, w * m + w), dst=ap(dstname, w * (m - 1), w * m)))
-            sent[0] += sum(len(e) for e in engs)
-            g.remote_dma_fused(tr, local_sem=T.sem.loc)
-        i = note({"G": (0.5, go)}, [(src, w, 4 * w)], [])
-        total = 0
-        for m in (1, 2, 3):
-            for s in range(n_ranks):
-                if target(s, t, m, n_ranks) == rank:
-                    ds = [cores[target(s, t, x, n_ranks)] for x in (1, 2, 3)]
-                    total += len(engine_split(topo, cores[s], ds)[m - 1])
-        note({"N": (2.6 if w > 8 else 1.9, None)}, [], [(dstname, 0, 3 * w)], sem="%s%d" % (kind, t), val=total, after=i)
+            for call in calls(rank):
+                tr = []
+                for m, engs in call.items():
+                    rid, pid = topo.addr(cores[target(rank, t, m, n_ranks)])[:2]
+                    tr.append(RemoteDMATransfer(dst_ids=[DstId(rid=rid, pnc=pid)], dma_engine_mask=sum(1 << e for e in engs),
+                                                remote_sem=T.sem["%s%d" % (kind, t)],
+                                                src=ap(src, w * m, w * m + w), dst=ap(dstname, w * (m - 1), w * m)))
+                    sent[0] += len(engs)
+                g.remote_dma_fused(tr, local_sem=T.sem.loc)
+        i = note({"G": (0.5, go)}, [(src, w * m, w * m + w) for m in ms], [])
+        got = landing.setdefault((kind, t), [0, []])
+        got[0] += sum(len(call[m]) for r in range(n_ranks) for call in calls(r) for m in call if target(r, t, m, n_ranks) == rank)
+        got[1].append(i)
+        if 3 in ms:
+            note({"N": (2.4 if w > 8 else 1.9, None)}, [], [(dstname, 0, 3 * w)], sem="%s%d" % (kind, t), val=got[0], after=got[1])
 
     def col(j, part=1):
         return ("DC", j, j + 1, part) if part != 1 else ("DC", j, j + 1)
@@ -227,31 +225,22 @@ def rank_program(g, core, T, topo):
     lo, hi = (0, 64), (64, 128)
 
     dma("Y", "ldx", ("XT", 0, 4096), T.x[:], 5.5)
-    dma("S", "ldc", ("CBI", 0, 512), T.cb[:], 3.0)
-    dma("Y", "ldp0", ("PK", 0, 1024), T.pk[:, 0:1024], 7.5)
-    dma("Y", "ldp1", ("PK", 1024, 2048), T.pk[:, 1024:2048], 9.5)
-    dma("S", "ldw", ("WTI", 0, 1), T.wt[:], 3.0)
+    first = [dma("S", "ldc", ("CBI", 0, 512), T.cb[:], 3.0)]
+    dma("Y", "ldp0", ("PK", 0, 1024), T.pk[:, 0:1024], 4.4, first)
+    dma("Y", "ldp1", ("PK", 1024, 2048), T.pk[:, 1024:2048], 6.2, first)
+    dma("Y", "ldw", ("WTI", 0, 1), T.wt[:], 6.4, first)
 
     iota(("PI", 0, 1), [[0, 1]], 0, 1)
-    iota(("IOF", 0, 256), [[1, 256]], 0, 0)
-    iota(("C2", 0, 128), [[0, 2], [2, 64]], 0, 0)
+    iota(("IOF", 0, 144), [[1, 144]], 0, 0)
+    iota(("C2", 0, 64), [[2, 64]], 0, 0)
     iota(("QI", 0, 512), [[0, 64], [8, 8]], -27, 0)
     fill(sq("ONE"), 1.0)
     fill(sq("CC"), 18.0)
-    fill(("CC", 0, 8, (0, 32)), 18.25)
-    for j, mask in enumerate((15, 112, 126, 1)):
+    for j, mask in enumerate((112, 126, 1)):
         ts(("PI", j + 1, j + 2), ("PI", 0, 1), mask, ALU.bitwise_and)
-    cp(("PF", 0, 5), ("PI", 0, 5))
-    p, zone, g16, even, odd = [pf(j) for j in range(5)]
+    cp(("PF", 0, 4), ("PI", 0, 4))
+    p, g16, even, odd = [pf(j) for j in range(4)]
     ts(sq("IDB"), sq("IOF"), p, ALU.is_equal)
-    ts(("RM", 0, 16), ("IOF", 0, 16), zone, ALU.is_equal)
-    ts(col(3), g16, 0.0625, ALU.mult, 128.0, ALU.add)
-    ts(("QB", 0, 256), ("IOF", 0, 256), col(3), ALU.is_equal)
-    for k in range(15):
-        lin(("DX", 128 * k, 128 * k + 128), ("QB", 120 - 8 * k, 248 - 8 * k), ("RM", k, k + 1))
-    ts(col(4), p, 2.0, ALU.mult)
-    ts(("DU", 0, 128), sq("C2"), col(4), ALU.is_equal)
-    ts(("DU", 128, 256), sq("C2"), 128.0, ALU.add, col(4), ALU.is_equal)
     for m in ORDER:
         cp(("C0", 128 * m, 128 * m + 128), ("CBI", m, 512, 4))
     fill(col(0, lo), -1792.0)
@@ -261,19 +250,21 @@ def rank_program(g, core, T, topo):
     ts(("MK", 0, 512), ("QI", 0, 512), col(1), ALU.mult, -2.0, ALU.add)
     for half in (lo, hi):
         pick(("MK", 0, 512, half), ("MK", 0, 512, half), [[-8, 8], [-1, 8], [0, 8]], 0)
-    lin(("D0", 0, 512), ("QI", 0, 512), 2.0 ** 18, -2.0 ** 20 - 512)
+    lin(("D0", 0, 512), ("QI", 0, 512), 2.0 ** 18, -2.0 ** 20 - 510)
     ts(col(2), odd, 511.0, ALU.mult, 1.0, ALU.add)
     ts(("PR", 0, 64), ("C2", 0, 64), even, ALU.is_equal, col(2), ALU.mult)
     for b in range(2):
-        fill(("SO", 1024 * b, 1024 * b + 64), 51.75 * 2 ** 18 - 3584)
+        fill(("SO", 1024 * b, 1024 * b + 64), LAST)
     ts(sq("I32"), sq("IOF"), p, ALU.is_equal)
     ts(sq("RZ"), sq("IOF"), 16.0, ALU.mult, p, ALU.is_equal)
-    ts(col(5), p, 7.5, ALU.is_gt, -256.0, ALU.mult)
+    lin(sq("NZ"), sq("IDB"), -255.0)
+    ts(col(5), p, 7.5, ALU.is_gt, -512.0, ALU.mult)
     fill(col(6), 0.0)
-    fill(col(6, (0, 2)), 608.0)
-    fill(col(6, (0, 1)), -199.0 * 2 ** 13)
-    ts(sq("NZ"), sq("IDB"), col(5), ALU.mult, col(6), ALU.add)
-    lin(sq("NR"), sq("IDB"), -512.0)
+    fill(col(6, (0, 3)), 121.0 / 512)
+    fill(col(6, (0, 2)), 4.5)
+    fill(col(6, (0, 1)), -199.0 * 64)
+    ts(sq("NR"), sq("IDB"), col(5), ALU.mult, col(6), ALU.add)
+    fill(("NR", 0, 8, (0, 1)), -207.0 * 64)
     pick(sq("PM"), sq("ONE"), [[-1, 8], [-8, 16]], 0)
     pick(sq("PS"), sq("ONE"), [[-1, 8], [-8, 16]], 8)
     tt(sq("DF"), sq("PM"), sq("PS"), ALU.subtract)
@@ -283,7 +274,7 @@ def rank_program(g, core, T, topo):
     ts(("S1", 0, 143), ("IOF", 0, 143), -15.0, ALU.add, g16, ALU.is_equal)
     cp(("WTF", 0, 1), ("WTI", 0, 1))
     lin(("LW", 0, 143), ("S1", 0, 143), ("WTF", 0, 1))
-    iota(("SI", 0, 32), [[16, 32]], 8192, 1)
+    iota(("SI", 0, 32), [[16, 32]], -512, 1)
     iota(("II", 0, 32), [[1, 4], [64, 8]], 0, 4)
     ts(col(10), g16, 4.0, ALU.mult)
     ts(("II", 0, 32), ("II", 0, 32), col(10), ALU.subtract)
@@ -293,7 +284,7 @@ def rank_program(g, core, T, topo):
         ts(("BT", 512 + c, 1536 + c), ("PK", c, c + 1024), 4095, ALU.bitwise_and)
         ts(("BT", 2560 + c, 3584 + c), ("PK", c, c + 1024), 12, ALU.logical_shift_right)
     cur[0] = "c"
-    fill(("DB", 0, 2048), 1.0)
+    iota(("DB", 0, 2048), [[0, 2048]], 1, 0)
     pick(("DB", 0, 2048), ("DB", 0, 2048), [[255, 16], [-16, 8], [-256, 16]], 0)
     lin(sq("PP"), sq("IDB"), 2048.0)
     lin(sq("PN"), sq("IDB"), -2048.0)
@@ -305,7 +296,7 @@ def rank_program(g, core, T, topo):
         def wrapped(a, b):
             for c, mat, src in ((0, "LW", V), (32, "S1", "SG")):
                 mms([(("x0", c + a, c + b), (mat, 15 - r, 143 - r), (src, 16 * a + r, 16 * b, 16)) for r in range(16)])
-            ts(Y(2, a, b), ("x0", 32 + a, 32 + b), -3.0, ALU.is_gt, 4096.0, ALU.mult)
+            ts(Y(2, a, b), ("x0", 32 + a, 32 + b), -3.0, ALU.is_gt, 8192.0, ALU.mult)
             tt(Y(3, a, b), Y(2, a, b), ("II", a, b), ALU.add)
 
         def places(a, b):
@@ -320,19 +311,18 @@ def rank_program(g, core, T, topo):
             m = ORDER[q]
             s0, j0, z0, o0 = 128 * m, 2048 * m, 256 * q, 1024 * (q % 2)
             X, D = BANKS[q % 2], BANKS[2 + 2 * (q % 3):4 + 2 * (q % 3)]
-            for c in range(0, 128, ECH):
-                cur[0] = "x%d" % q
-                for a in range(s0 + c, s0 + c + ECH, XCH):
-                    gather(("G", 16 * a, 16 * (a + XCH)), ("XT", 0, 4096), (C, a, a + XCH))
-                cur[0] = "e%d" % q
-                ja, jb = j0 + 16 * c, j0 + 16 * (c + ECH)
-                mms([((X, c, c + ECH), sq("CC"), ("ONE", 0, ECH))] +
-                    [((X, c, c + ECH), ("DX", 128 * k, 128 * k + 128), ("G", ja + k, jb, 16)) for k in range(15)])
+            cur[0] = "x%d" % q
+            for a in range(s0, s0 + 128, XCH[q]):
+                gather(("G", 16 * a, 16 * (a + XCH[q])), ("XT", 0, 4096), (C, a, a + XCH[q]))
+            cur[0] = "e%d" % q
+            mms([(sq(X), sq("ONE"), sq("CC"))] +
+                [((X, 8 * k + 8, 8 * k + 16), ("G", j0 + k, j0 + 2048, 16), ("IDB", k, 128, 16)) for k in range(15)])
             cur[0] = "t%d" % q
             th, z = ("TH", s0, s0 + 128), ("Z", s0, s0 + 128)
             lin(th, sq(X), 1.0, -7.5)
             tt(z, sq(X), th, ALU.subtract)
-            mms([((X, 128 + 128 * b, 256 + 128 * b), ("DU", 128 * b, 128 * b + 128), z) for b in range(2)], groups=1)
+            mms([((X, 128 + 128 * b, 256 + 128 * b, half), ("Z", s0 + 64 * b, s0 + 64 * b + 64), sq("IDB"))
+                 for b in range(2) for half in (lo, hi)], groups=1)
             sa(("U", z0, z0 + 256), (X, 128, 384), AF.Square, scale=256.0, bias=col(0))
             for b in range(2):
                 c = 64 * (1 - b)
@@ -345,9 +335,9 @@ def rank_program(g, core, T, topo):
                 scan(("SO", o0 + 512 * b + c, o0 + 512 * b + 512), ("D0", c, 512), (D[b], c, 512))
             cur[0] = "v%d" % q
             so, rr, vp, vq = ("SO", o0 + 7, o0 + 1024, 8), ("RR", s0, s0 + 128), ("VP", s0, s0 + 128), (V, s0, s0 + 128)
-            mms([(sq(D[0]), sq("NZ"), z), (sq(D[0]), so, sq("I32"))])
-            mms([(sq(D[1]), sq("NZ"), z), (sq(D[1]), sq("RZ"), ("G", j0, j0 + 2048, 16)), (sq(D[1]), so, sq("I32"))], last=False)
-            lin(rr, sq(D[0]), 2.0 ** -9, -2.5 + 2.0 ** -10)
+            mms([(sq(D[0]), z, sq("NZ")), (sq(D[0]), so, sq("I32"))])
+            mms([(sq(D[1]), z, sq("NZ")), (sq(D[1]), sq("RZ"), ("G", j0, j0 + 2048, 16)), (sq(D[1]), so, sq("I32"))], last=False)
+            lin(rr, sq(D[0]), 2.0 ** -9, 1024 - LAST / 512)
             mms([(sq(D[1]), sq("NR"), rr)], first=False)
             tt(vp, sq(D[1]), rr, ALU.max)
             mms([((D[0], 128, 256), sq("DF"), vp)])
@@ -355,9 +345,10 @@ def rank_program(g, core, T, topo):
             sa(("AB", s0, s0 + 128), (D[0], 128, 256), AF.Abs)
             sa(("SG", s0, s0 + 128), ("AB", s0, s0 + 128), AF.Sign, bias=-64.5, acc=("ACC", q, q + 1))
             lin(vq, (D[1], 128, 256), 1.0, -1280.0)
-            if q == 2:
+            if m:
                 cur[0] = "vin"
-                send(t, "vin", V, 128, "VIN%d" % t)
+                send(t, "vin", V, 128, "VIN%d" % t, (m,))
+            if q == 2:
                 cur[0] = "h"
                 ts(("ACC", 4, 5), ("ACC", 0, 1), ("ACC", 1, 2), ALU.add, ("ACC", 2, 3), ALU.add)
                 wrapped(8, 32)
@@ -370,13 +361,12 @@ def rank_program(g, core, T, topo):
         wrapped(0, 8)
         places(0, 8)
         ts(Y(5), ("x0", 0, 32), 37.0, ALU.mult, acol, ALU.add)
-        ts(Y(7), ("x0", 32, 64), -3.0, ALU.is_lt, 8704.0, ALU.mult)
         ts(Y(6), Y(5), 4095, ALU.bitwise_and)
-        tt(Y(8), Y(6), Y(7), ALU.add)
-        tt(Y(9), Y(8), ("SI", 0, 32), ALU.max)
-        ts((NX, 0, 32), Y(9), -8192.0, ALU.add)
+        tt(Y(7), Y(6), Y(2), ALU.subtract)
+        tt(Y(8), Y(7), ("SI", 0, 32), ALU.max)
+        ts((NX, 0, 32), Y(8), 512.0, ALU.add)
         cur[0] = "m"
-        ts(("CF", 0, 512), (C, 0, 512), -2048.0, ALU.add)
+        lin(("CF", 0, 512), (C, 0, 512), 1.0, -2048.0)
         mms([(("d4", 0, 512), sq("IDB"), ("CF", 0, 512)), (("d4", 0, 512), sq("PN"), ("SG", 0, 512))])
         lin(("X2S", 0, 512), ("d4", 0, 512), 1.0)
         for q in range(4):
@@ -384,21 +374,21 @@ def rank_program(g, core, T, topo):
             for a in range(128 * ORDER[q], 128 * ORDER[q] + 128, ECH):
                 b = a + ECH
                 cur[0] = "b%d" % q
-                for c in range(a, b, BCH):
-                    gather(("GB", 16 * c, 16 * (c + BCH)), ("BT", 512, 4608), (C, c, c + BCH), bias=-2048.0)
+                for c in range(a, b, BCH[q]):
+                    gather(("GB", 16 * c, 16 * (c + BCH[q])), ("BT", 512, 4608), (C, c, c + BCH[q]), bias=-2048.0)
                 cur[0] = "m%d" % q
                 mms([((M, a, b), ("DB", 128 * k, 128 * k + 128), ("GB", 16 * a + k, 16 * b, 16)) for k in range(1, 16)]
                     + [((M, a, b), sq("PP"), ("SG", a, b))])
             tt(("BT", b - 128, b), (M, b - 128, b), ("X2S", b - 128, b), ALU.max)
         cur[0] = "o"
-        scatter(("XT", 0, 8192), (OF, 0, 8), (V, 0, 128))
-        scatter(("BT", 512, 8704), (OF, 0, 8), (C, 0, 128))
+        scatter(("XT", 0, 12288), (OF, 0, 8), (V, 0, 128))
+        scatter(("BT", 512, 12800), (OF, 0, 8), (C, 0, 128))
         cur[0] = "z"
-        scatter(("BT", 512, 8704), ("OIN%d" % t, 0, 24), ("CIN%d" % t, 0, 384))
-        scatter(("XT", 0, 8192), ("OIN%d" % t, 0, 24), ("VIN%d" % t, 0, 384))
+        scatter(("BT", 512, 12800), ("OIN%d" % t, 0, 24), ("CIN%d" % t, 0, 384))
+        scatter(("XT", 0, 12288), ("OIN%d" % t, 0, 24), ("VIN%d" % t, 0, 384))
         for m in ORDER:
             out = ("C%d" % (t + 1), 128 * m, 128 * m + 128) if t + 1 < NR else ("YC", m, 512, 4)
-            gather(out, ("BT", 0, 4608), (NX, 8 * m, 8 * m + 8), both=False)
+            gather(out, ("BT", 0, 4608), (NX, 8 * m, 8 * m + 8))
 
     cur[0] = "st"
     dma("Y", "stx", T.yx[:], ("XT", 0, 4096), 5.5)
@@ -454,58 +444,97 @@ def improve(ops, seq):
             if o["deps"][j] and j not in above[i]:
                 hard[i].append(j)
                 above[i] |= above[j] | {j}
-    dur = [{q: d for q, (d, _) in o["alts"].items()} for o in ops]
-    lat = [o["lat"] for o in ops]
-    start, why = [0.0] * n, [-1] * n
+    durs = [[{q: d + o["ind"] * (r - 1) for q, (d, _) in o["alts"].items()} for o in ops] for r in RATES]
+    lat = [o["lat"] + WAKE for o in ops]
+    heads = [i for i, o in enumerate(ops) if o["tag"] == "cin" and "G" in o["alts"]]
+    size = heads[1] - heads[0]
+    first, last = heads[0], heads[0] + NR * size
+    marks = [{i: 0.0 for i in range(first + size - 4, last, size)} for r in RATES]
+    ends = [[0.0] * n for r in RATES]
 
-    def clock():
-        end, free, last = [0.0] * n, dict.fromkeys("GNPSVY", 0.0), dict.fromkeys("GNPSVY", -1)
+    def clock(slack):
+        for dur, end, mark in zip(durs, ends, marks):
+            free = {"G": 0.0, "P": 0.0, "S": 0.0, "V": 0.0, "Y": 0.0, "N": 0.0}
+            for i in order:
+                q = qof[i]
+                st = free[q]
+                for j in hard[i]:
+                    e = end[j] - NEAR if qof[j] == q else end[j]
+                    if e > st:
+                        st = e
+                st += dur[i][q]
+                if q != "N":
+                    free[q] = st
+                end[i] = st + lat[i]
+                if i in mark and st > mark[i] + slack:
+                    return 1e9
+        return sum(max(end) for end in ends) / len(ends)
+
+    def remember():
+        for end, mark in zip(ends, marks):
+            mark.update({i: end[i] - lat[i] for i in mark})
+
+    def critical(dur, end):
+        start = [end[i] - lat[i] - dur[i][qof[i]] for i in range(n)]
+        order.sort(key=lambda i: start[i])
+        before, seen = {}, {}
         for i in order:
-            q = qof[i]
-            st, w = free[q], last[q]
-            for j in hard[i]:
-                e = end[j] + (SAME if qof[j] == q else WAKE)
-                if e > st:
-                    st, w = e, j
-            start[i], why[i] = st, w
-            st += dur[i][q]
-            if q != "N":
-                free[q], last[q] = st, i
-            end[i] = st + lat[i]
-        return max(end), end
+            before[i], seen[qof[i]] = seen.get(qof[i]), i
+        path = [end.index(max(end))]
+        while start[path[-1]] > 1e-6:
+            i = path[-1]
+            near = hard[i] + ([before[i]] if before[i] is not None and qof[i] != "N" else [])
+            path.append(max(near, key=lambda j: end[j] - (lat[j] if j not in hard[i] else NEAR if qof[j] == qof[i] else 0)))
+        return path
 
-    rnd = np.random.RandomState(SEED).random_sample((MOVES, 6)).tolist()
-    now = clock()[0]
+    def move(i, j, behind, q):
+        p, r = order.index(i), order.index(j)
+        to = r + behind - (r > p)
+        if any(x in ops[i]["deps"] for x in order[to:p]) or any(x in users[i] for x in order[p + 1:to + 1]):
+            return []
+        was, qof[i] = qof[i], q
+        order.insert(to, order.pop(p))
+        return [(i, p, to, was)]
+
+    now = clock(1e9)
     best = (now, list(order), list(qof))
-    for it, (r0, r1, r2, r3, r4, r5) in enumerate(rnd):
+    for it, (r0, r1, r2, r3, r4, r5, r6) in enumerate(np.random.RandomState(SEED).random_sample((MOVES, 7)).tolist()):
         if it % 50 == 0:
-            total, end = clock()
-            path = [end.index(total)]
-            while why[path[-1]] >= 0:
-                path.append(why[path[-1]])
-            order.sort(key=lambda i: start[i])
+            clock(1e9)
+            remember()
+            path = critical(durs[it // 50 % len(RATES)], ends[it // 50 % len(RATES)])
         p = order.index(path[int(r1 * len(path))]) if r0 < 0.6 else int(r1 * n)
         if r0 < 0.3:
             p = min(n - 1, max(0, p + int(r0 * 80) - 12))
         i, span = order[p], (4, 10, 25, 60)[int(r2 * 4)]
-        was = qof[i]
-        if len(dur[i]) > 1 and r3 < 0.4:
-            qof[i] = "S" if was == "V" else "V"
+        q = qof[i]
+        if len(ops[i]["alts"]) > 1 and r3 < 0.4:
+            q = "S" if q == "V" else "V"
         a = b = p
         while a > 0 and p - a < span and order[a - 1] not in ops[i]["deps"]:
             a -= 1
         while b < n - 1 and b - p < span and order[b + 1] not in users[i]:
             b += 1
         to = a + int(r4 * (b - a + 1))
-        order.insert(to, order.pop(p))
-        total = clock()[0]
-        if total <= now - (HEAT * (1 - it / MOVES) + 0.003) * math.log(r5 + 1e-12):
+        if to == p and (p == 0 or q == qof[i]):
+            continue
+        j, behind = (order[to], to > p) if to != p else (order[p - 1], True)
+        done = move(i, j, behind, q)
+        if r6 < TWINS and first <= i < last and first <= j < last:
+            for d in range(-2 * size, 3 * size, size):
+                if d and first <= i + d < last and first <= j + d < last:
+                    done += move(i + d, j + d, behind, q)
+        slack = -(HEAT * (1 - it / MOVES) + 0.003) * math.log(r5 + 1e-12)
+        total = clock(len(RATES) * slack + 0.3)
+        if total <= now + slack:
             now = total
+            remember()
             if now < best[0]:
                 best = (now, list(order), list(qof))
         else:
-            order.insert(p, order.pop(to))
-            qof[i] = was
+            for i, p, to, was in reversed(done):
+                order.insert(p, order.pop(to))
+                qof[i] = was
     return [(i, best[2][i]) for i in best[1]]
 
 

import math
import numpy as np
from concourse.bass import DstId, RemoteDMATransfer
from concourse.mybir import AluOpType as ALU, ActivationFunctionType as AF

NR = 3
ORDER = [1, 2, 3, 0]
XCH = (64, 64, 64, 64)
BCH = (32, 32, 64, 64)
ECH = 64
LAST = 51.75 * 2 ** 18 - 3570
LOOK = 0.15
BON = {"u": 6.0}
CY, GA, SC, TE, VF, SF, WAKE, NEAR = 0.00083, 1.56, 3.8, 0.00043, 0.055, 0.07, 0.12, 0.06
RATES = (1.0,)
MOVES, HEAT, TWINS, SEED = 240000, 0.15, 0.85, 1
PLAN = []

SCRATCH = {}
for _spec in (
        "XT 12288 bfloat16, BT 12800 int32, PK 2048 int32, CBI 512 int32, WTI 1 int32, WTF 1 float32, G 8192 bfloat16, "
        "GB 8192 float16, CF 512 float16, TH 512 bfloat16, Z 512 bfloat16, U 1024 bfloat16, SO 2048 float32, "
        "RR 512 float16, VP 512 float16, AB 512 bfloat16, SG 512 bfloat16, ACC 8 float32, X2S 512 float32, YW 320 int32, "
        "YC 512 float32, SI 32 int32, II 32 int32, PI 8 int32, PF 8 float32, DC 24 float32, IOF 144 float32, "
        "C2 128 float32, QI 512 bfloat16, D0 512 float32, MK 512 bfloat16, GI 128 float32, "
        "S1 144 bfloat16, LW 144 bfloat16, RZ 128 bfloat16, IDB 128 bfloat16, I32 128 float32, "
        "PR 64 bfloat16, NZ 128 bfloat16, NR 128 bfloat16, "
        "PM 128 bfloat16, PS 128 bfloat16, DF 128 bfloat16, BO 128 float32, CC 128 bfloat16, ONE 128 bfloat16, "
        "DB 2048 bfloat16, PP 128 bfloat16, PN 128 bfloat16").split(", ") + [
        "%s%d %s" % (n, t, d) for t in range(NR) for n, d in (
            ("C", "512 uint16"), ("V", "512 bfloat16"), ("OF", "32 uint16"), ("NX", "32 uint16"),
            ("CIN", "384 uint16"), ("VIN", "384 bfloat16"), ("OIN", "24 uint16"))]:
    _n, _w, _d = _spec.split()
    SCRATCH[_n] = ("sbuf", [128, int(_w)], _d)
BANKS = ["x0", "x1", "d0", "d1", "d2", "d3", "d4", "d5"]
for _n in BANKS:
    SCRATCH[_n] = ("psum", [128, 512], "float32")
DMAS = ["ldc", "ldw", "ldx", "ldp0", "ldp1", "stx", "stc"]
SEMAPHORES = ["qV", "qS", "qP", "qG", "loc"] + DMAS + ["%s%d" % (n, t) for n in ("cin", "vin", "oin") for t in range(NR)]


def shares(pool, n):
    z = len(pool)
    sizes = {1: [z], 2: [z // 2] * 2, 3: [z // 2, z // 4, z // 4]}[n]
    return [pool[sum(sizes[:i]):sum(sizes[:i + 1])] for i in range(n)]


def engine_split(topo, src, dsts):
    lists = {m: topo.engines(src, d) for m, d in dsts.items()}
    pool = min(lists.values(), key=len)
    narrow = [m for m in dsts if len(lists[m]) == len(pool)]
    wide = [m for m in dsts if len(lists[m]) > len(pool)]
    if len(narrow) == 3 and topo.chip(dsts[narrow[0]]) != topo.chip(src):
        return [dict(zip(narrow, shares(pool, 2))), {narrow[2]: pool}]
    got = dict(zip(narrow, shares(pool, len(narrow))))
    if wide:
        got.update(zip(wide, shares([e for e in lists[wide[0]] if e not in pool], len(wide))))
    return [got]


def target(r, t, m, n):
    return (r + 1 + ((t + m - 1) % (n - 1))) % n


def rank_program(g, core, T, topo):
    rank = T.rank_of(core)
    if rank is None:
        return
    cores = list(T.cores)
    n_ranks = len(cores)
    ops, hist, sent, cur, landing = [], {}, [0], ["c"], {}
    vec, act, ten = g.vector, g.scalar, g.tensor

    def note(alts, rd, wr, sem=None, val=0, after=(), lat=0.0, ind=0.0):
        idx = len(ops)
        pe = "P" in alts
        deps = {}
        for w, regs in ((0, rd), (1, wr)):
            for reg in regs:
                b, c0, c1 = reg[0], reg[1], reg[2]
                ps = b in BANKS
                keep = []
                for e in hist.get(b, []):
                    j, ew, e0, e1 = e
                    if j == idx:
                        keep.append(e)
                        continue
                    if ps or (e0 < c1 and c0 < e1 and (ew or w)):
                        deps[j] = not (pe and "P" in ops[j]["alts"])
                    if ps and pe:
                        continue
                    if w and not ps and len(reg) == 3 and c0 <= e0 and e1 <= c1:
                        continue
                    keep.append(e)
                keep.append((idx, w, c0, c1))
                hist[b] = keep
        deps.update(dict.fromkeys(after, True))
        ops.append({"alts": alts, "deps": deps, "sem": sem, "val": val, "lat": lat, "ind": ind, "tag": cur[0]})
        return idx

    def ap(b, c0, c1, x=1):
        t = T[b]
        if isinstance(x, tuple):
            return t[x[0]:x[1], c0:c1]
        return t[:, c0:c1] if x == 1 else t[:, c0:c1:x]

    def width(r):
        return -((r[1] - r[2]) // r[3]) if len(r) > 3 and not isinstance(r[3], tuple) else r[2] - r[1]

    def narrow(*regs):
        return all(SCRATCH[r[0]][2] in ("bfloat16", "float16", "uint16") for r in regs)

    def val(x):
        return ap(*x) if isinstance(x, tuple) else x

    def v_ts(out, in0, s1, op0, s2=None, op1=None):
        def go():
            if op1 is None:
                return vec.tensor_scalar(ap(*out), ap(*in0), val(s1), None, op0)
            return vec.tensor_scalar(ap(*out), ap(*in0), val(s1), val(s2), op0, op1)
        return VF + width(out) * CY * (0.5 if narrow(out, in0) else 1), go

    def s_act(out, in_, func, scale=None, bias=None, acc=None):
        def go():
            kw = {n: val(x) for n, x in (("scale", scale), ("bias", bias), ("accum_out", acc)) if x is not None}
            return act.activation(ap(*out), ap(*in_), func, **kw)
        return SF + width(out) * CY, go

    def cols(*xs):
        return [x for x in xs if isinstance(x, tuple)]

    def ts(out, in0, s1, op0, s2=None, op1=None):
        note({"V": v_ts(out, in0, s1, op0, s2, op1)}, [in0] + cols(s1, s2), [out])

    def sa(out, in_, func, scale=None, bias=None, acc=None):
        note({"S": s_act(out, in_, func, scale, bias, acc)}, [in_] + cols(scale, bias), [out] + cols(acc))

    def lin(out, in_, scale, bias=0.0):
        note({"V": v_ts(out, in_, scale, ALU.mult, bias, ALU.add), "S": s_act(out, in_, AF.Copy, scale, bias)},
             [in_] + cols(scale), [out])

    def tt(out, in0, in1, op):
        both = in0[0] not in BANKS and in1[0] not in BANKS
        go = lambda: vec.tensor_tensor(ap(*out), ap(*in0), ap(*in1), op)
        note({"V": (VF + width(out) * CY * (2 if both else 1), go)}, [in0, in1], [out])

    def cp(out, in_):
        note({"V": (VF + width(out) * CY, lambda: vec.tensor_copy(ap(*out), ap(*in_)))}, [in_], [out])

    def fill(reg, x):
        note({"V": (VF + width(reg) * CY * (0.5 if narrow(reg) else 1), lambda: vec.memset(ap(*reg), x))}, [], [reg])

    def scan(out, d0, d1):
        go = lambda: vec.tensor_tensor_scan(ap(*out), ap(*d0), ap(*d1), 0.0, ALU.add, ALU.max)
        note({"V": (VF + width(out) * CY, go)}, [d0, d1], [out])

    def mms(items, first=True, last=True, groups=None):
        def flags(i):
            if groups:
                return i % groups == 0, i % groups == groups - 1
            return first and i == 0, last and i == len(items) - 1

        def go():
            for i, (o, l, r) in enumerate(items):
                ins = ten.matmul(ap(*o), ap(*l), ap(*r), *flags(i))
            return ins
        dur = sum(TE * max(64, width(r)) * (4 if SCRATCH[r[0]][2] == "float32" else 1) for o, l, r in items)
        note({"P": (dur, go)}, [x for o, l, r in items for x in (l, r)], [o for o, l, r in items], lat=0.05)

    def iota(out, pattern, base, cm):
        go = lambda: g.iota(ap(*out), pattern, base, cm, allow_small_or_imprecise_dtypes=SCRATCH[out[0]][2] != "int32")
        note({"G": (0.13 + 2 * width(out) * CY, go)}, [], [out])

    def pick(out, in_, pattern, base):
        go = lambda: g.affine_select(ap(*out), ap(*in_), pattern, ALU.is_equal, 0.0, base, 1)
        note({"G": (0.17 + 2 * width(out) * CY, go)}, [in_], [out])

    def dma(q, sem, out, src, us, after=()):
        eng = g.sync if q == "Y" else act
        go = lambda: eng.dma_start(val(out), val(src))
        return note({q: (0.06, go)}, cols(src), cols(out), sem=sem, val=16, lat=us, after=after)

    def gather(out, win, lst, bias=0.0):
        n = 16 * (lst[2] - lst[1])
        w = lambda: ap(*win).indirect(ap(*lst))
        on_v = lambda: vec.tensor_scalar(ap(*out), w(), bias, None, ALU.add) if bias else vec.tensor_copy(ap(*out), w())
        on_s = lambda: act.activation(ap(*out), w(), AF.Copy, bias=bias)
        note({"V": (VF + n * CY * GA, on_v), "S": (SF + n * CY * GA, on_s)}, [win, lst], [out], ind=n * CY * GA)

    def scatter(win, lst, src):
        n = 16 * (lst[2] - lst[1])
        go = lambda: vec.tensor_copy(ap(*win).indirect(ap(*lst)), ap(*src))
        note({"V": (VF + n * CY * SC, go)}, [lst, src], [win], ind=n * CY * SC)

    def send(t, kind, src, w, dstname, ms=(1, 2, 3)):
        def calls(r):
            return engine_split(topo, cores[r], {m: cores[target(r, t, m, n_ranks)] for m in ms})

        def go():
            for call in calls(rank):
                tr = []
                for m, engs in call.items():
                    rid, pid = topo.addr(cores[target(rank, t, m, n_ranks)])[:2]
                    tr.append(RemoteDMATransfer(dst_ids=[DstId(rid=rid, pnc=pid)], dma_engine_mask=sum(1 << e for e in engs),
                                                remote_sem=T.sem["%s%d" % (kind, t)],
                                                src=ap(src, w * m, w * m + w), dst=ap(dstname, w * (m - 1), w * m)))
                    sent[0] += len(engs)
                g.remote_dma_fused(tr, local_sem=T.sem.loc)
        i = note({"G": (0.5, go)}, [(src, w * m, w * m + w) for m in ms], [])
        got = landing.setdefault((kind, t), [0, []])
        got[0] += sum(len(call[m]) for r in range(n_ranks) for call in calls(r) for m in call if target(r, t, m, n_ranks) == rank)
        got[1].append(i)
        if 3 in ms:
            note({"N": (2.4 if w > 8 else 1.9, None)}, [], [(dstname, 0, 3 * w)], sem="%s%d" % (kind, t), val=got[0], after=got[1])

    def col(j, part=1):
        return ("DC", j, j + 1, part) if part != 1 else ("DC", j, j + 1)

    def pf(j):
        return ("PF", j, j + 1)

    def sq(name):
        return (name, 0, 128)

    lo, hi = (0, 64), (64, 128)

    dma("Y", "ldx", ("XT", 0, 4096), T.x[:], 5.5)
    first = [dma("S", "ldc", ("CBI", 0, 512), T.cb[:], 3.0)]
    dma("Y", "ldp0", ("PK", 0, 1024), T.pk[:, 0:1024], 4.4, first)
    dma("Y", "ldp1", ("PK", 1024, 2048), T.pk[:, 1024:2048], 6.2, first)
    dma("Y", "ldw", ("WTI", 0, 1), T.wt[:], 6.4, first)

    iota(("PI", 0, 1), [[0, 1]], 0, 1)
    iota(("IOF", 0, 144), [[1, 144]], 0, 0)
    iota(("C2", 0, 64), [[2, 64]], 0, 0)
    iota(("QI", 0, 512), [[0, 64], [8, 8]], -27, 0)
    fill(sq("ONE"), 1.0)
    fill(sq("CC"), 18.0)
    for j, mask in enumerate((112, 126, 1)):
        ts(("PI", j + 1, j + 2), ("PI", 0, 1), mask, ALU.bitwise_and)
    cp(("PF", 0, 4), ("PI", 0, 4))
    p, g16, even, odd = [pf(j) for j in range(4)]
    ts(sq("IDB"), sq("IOF"), p, ALU.is_equal)
    for m in ORDER:
        cp(("C0", 128 * m, 128 * m + 128), ("CBI", m, 512, 4))
    fill(col(0, lo), -1792.0)
    fill(col(0, hi), -2048.0)
    fill(col(1, lo), 1.0)
    fill(col(1, hi), -1.0)
    ts(("MK", 0, 512), ("QI", 0, 512), col(1), ALU.mult, -2.0, ALU.add)
    for half in (lo, hi):
        pick(("MK", 0, 512, half), ("MK", 0, 512, half), [[-8, 8], [-1, 8], [0, 8]], 0)
    lin(("D0", 0, 512), ("QI", 0, 512), 2.0 ** 18, -2.0 ** 20 - 510)
    ts(col(2), odd, 511.0, ALU.mult, 1.0, ALU.add)
    ts(("PR", 0, 64), ("C2", 0, 64), even, ALU.is_equal, col(2), ALU.mult)
    for b in range(2):
        fill(("SO", 1024 * b, 1024 * b + 64), LAST)
    ts(sq("I32"), sq("IOF"), p, ALU.is_equal)
    ts(sq("RZ"), sq("IOF"), 16.0, ALU.mult, p, ALU.is_equal)
    lin(sq("NZ"), sq("IDB"), -255.0)
    ts(col(5), p, 7.5, ALU.is_gt, -512.0, ALU.mult)
    fill(col(6), 0.0)
    fill(col(6, (0, 3)), 121.0 / 512)
    fill(col(6, (0, 2)), 4.5)
    fill(col(6, (0, 1)), -199.0 * 64)
    ts(sq("NR"), sq("IDB"), col(5), ALU.mult, col(6), ALU.add)
    fill(("NR", 0, 8, (0, 1)), -207.0 * 64)
    pick(sq("PM"), sq("ONE"), [[-1, 8], [-8, 16]], 0)
    pick(sq("PS"), sq("ONE"), [[-1, 8], [-8, 16]], 8)
    tt(sq("DF"), sq("PM"), sq("PS"), ALU.subtract)
    fill(("DF", 0, 128, 16), 0.0)
    iota(sq("GI"), [[16, 8], [0, 16]], 0, 0)
    ts(sq("BO"), sq("GI"), g16, ALU.is_equal, 0.5, ALU.mult)
    ts(("S1", 0, 143), ("IOF", 0, 143), -15.0, ALU.add, g16, ALU.is_equal)
    cp(("WTF", 0, 1), ("WTI", 0, 1))
    lin(("LW", 0, 143), ("S1", 0, 143), ("WTF", 0, 1))
    iota(("SI", 0, 32), [[16, 32]], -512, 1)
    iota(("II", 0, 32), [[1, 4], [64, 8]], 0, 4)
    ts(col(10), g16, 4.0, ALU.mult)
    ts(("II", 0, 32), ("II", 0, 32), col(10), ALU.subtract)
    ts(("SI", 0, 32), ("SI", 0, 32), g16, ALU.subtract)
    cur[0] = "u"
    for c in (0, 1024):
        ts(("BT", 512 + c, 1536 + c), ("PK", c, c + 1024), 4095, ALU.bitwise_and)
        ts(("BT", 2560 + c, 3584 + c), ("PK", c, c + 1024), 12, ALU.logical_shift_right)
    cur[0] = "c"
    iota(("DB", 0, 2048), [[0, 2048]], 1, 0)
    pick(("DB", 0, 2048), ("DB", 0, 2048), [[255, 16], [-16, 8], [-256, 16]], 0)
    lin(sq("PP"), sq("IDB"), 2048.0)
    lin(sq("PN"), sq("IDB"), -2048.0)

    for t in range(NR):
        C, V, OF, NX = "C%d" % t, "V%d" % t, "OF%d" % t, "NX%d" % t
        Y = lambda i, a=0, b=32: ("YW", 32 * i + a, 32 * i + b)

        def wrapped(a, b):
            for c, mat, src in ((0, "LW", V), (32, "S1", "SG")):
                mms([(("x0", c + a, c + b), (mat, 15 - r, 143 - r), (src, 16 * a + r, 16 * b, 16)) for r in range(16)])
            ts(Y(2, a, b), ("x0", 32 + a, 32 + b), -3.0, ALU.is_gt, 8192.0, ALU.mult)
            tt(Y(3, a, b), Y(2, a, b), ("II", a, b), ALU.add)

        def places(a, b):
            ts(Y(0, a, b), ("x0", a, b), acol, ALU.add, 512.0, ALU.mult)
            ts(Y(1, a, b), Y(0, a, b), 3584, ALU.bitwise_and)
            tt(Y(4, a, b), Y(1, a, b), Y(3, a, b), ALU.add)
            cp((OF, a, b), Y(4, a, b))

        cur[0] = "cin"
        send(t, "cin", C, 128, "CIN%d" % t)
        for q in range(4):
            m = ORDER[q]
            s0, j0, z0, o0 = 128 * m, 2048 * m, 256 * q, 1024 * (q % 2)
            X, D = BANKS[q % 2], BANKS[2 + 2 * (q % 3):4 + 2 * (q % 3)]
            cur[0] = "x%d" % q
            for a in range(s0, s0 + 128, XCH[q]):
                gather(("G", 16 * a, 16 * (a + XCH[q])), ("XT", 0, 4096), (C, a, a + XCH[q]))
            cur[0] = "e%d" % q
            mms([(sq(X), sq("ONE"), sq("CC"))] +
                [((X, 8 * k + 8, 8 * k + 16), ("G", j0 + k, j0 + 2048, 16), ("IDB", k, 128, 16)) for k in range(15)])
            cur[0] = "t%d" % q
            th, z = ("TH", s0, s0 + 128), ("Z", s0, s0 + 128)
            lin(th, sq(X), 1.0, -7.5)
            tt(z, sq(X), th, ALU.subtract)
            mms([((X, 128 + 128 * b, 256 + 128 * b, half), ("Z", s0 + 64 * b, s0 + 64 * b + 64), sq("IDB"))
                 for b in range(2) for half in (lo, hi)], groups=1)
            sa(("U", z0, z0 + 256), (X, 128, 384), AF.Square, scale=256.0, bias=col(0))
            for b in range(2):
                c = 64 * (1 - b)
                cur[0] = "p%d" % q
                mms([((D[b], 64 * kk, 64 * kk + 64), ("G", j0 + 8 * b + kk, j0 + 2048, 16), ("PR", 0, 64))
                     for kk in range(1 - b, 8)], last=False)
                cur[0] = "d%d" % q
                mms([((D[b], c, 512), ("U", z0 + 128 * b, z0 + 128 * b + 128), ("MK", c, 512))], first=False)
                cur[0] = "s%d" % q
                scan(("SO", o0 + 512 * b + c, o0 + 512 * b + 512), ("D0", c, 512), (D[b], c, 512))
            cur[0] = "v%d" % q
            so, rr, vp, vq = ("SO", o0 + 7, o0 + 1024, 8), ("RR", s0, s0 + 128), ("VP", s0, s0 + 128), (V, s0, s0 + 128)
            mms([(sq(D[0]), z, sq("NZ")), (sq(D[0]), so, sq("I32"))])
            mms([(sq(D[1]), z, sq("NZ")), (sq(D[1]), sq("RZ"), ("G", j0, j0 + 2048, 16)), (sq(D[1]), so, sq("I32"))], last=False)
            lin(rr, sq(D[0]), 2.0 ** -9, 1024 - LAST / 512)
            mms([(sq(D[1]), sq("NR"), rr)], first=False)
            tt(vp, sq(D[1]), rr, ALU.max)
            mms([((D[0], 128, 256), sq("DF"), vp)])
            mms([((D[1], 128, 256), sq("PM"), vp)])
            sa(("AB", s0, s0 + 128), (D[0], 128, 256), AF.Abs)
            sa(("SG", s0, s0 + 128), ("AB", s0, s0 + 128), AF.Sign, bias=-64.5, acc=("ACC", q, q + 1))
            lin(vq, (D[1], 128, 256), 1.0, -1280.0)
            if m:
                cur[0] = "vin"
                send(t, "vin", V, 128, "VIN%d" % t, (m,))
            if q == 2:
                cur[0] = "h"
                ts(("ACC", 4, 5), ("ACC", 0, 1), ("ACC", 1, 2), ALU.add, ("ACC", 2, 3), ALU.add)
                wrapped(8, 32)
        cur[0] = "a"
        acol = ("x1", 0, 1)
        mms([(acol, sq("BO"), ("ACC", q, q + 1)) for q in (4, 3)])
        places(8, 32)
        send(t, "oin", OF, 8, "OIN%d" % t)
        cur[0] = "n"
        wrapped(0, 8)
        places(0, 8)
        ts(Y(5), ("x0", 0, 32), 37.0, ALU.mult, acol, ALU.add)
        ts(Y(6), Y(5), 4095, ALU.bitwise_and)
        tt(Y(7), Y(6), Y(2), ALU.subtract)
        tt(Y(8), Y(7), ("SI", 0, 32), ALU.max)
        ts((NX, 0, 32), Y(8), 512.0, ALU.add)
        cur[0] = "m"
        lin(("CF", 0, 512), (C, 0, 512), 1.0, -2048.0)
        mms([(("d4", 0, 512), sq("IDB"), ("CF", 0, 512)), (("d4", 0, 512), sq("PN"), ("SG", 0, 512))])
        lin(("X2S", 0, 512), ("d4", 0, 512), 1.0)
        for q in range(4):
            M = BANKS[4 + q % 2]
            for a in range(128 * ORDER[q], 128 * ORDER[q] + 128, ECH):
                b = a + ECH
                cur[0] = "b%d" % q
                for c in range(a, b, BCH[q]):
                    gather(("GB", 16 * c, 16 * (c + BCH[q])), ("BT", 512, 4608), (C, c, c + BCH[q]), bias=-2048.0)
                cur[0] = "m%d" % q
                mms([((M, a, b), ("DB", 128 * k, 128 * k + 128), ("GB", 16 * a + k, 16 * b, 16)) for k in range(1, 16)]
                    + [((M, a, b), sq("PP"), ("SG", a, b))])
            tt(("BT", b - 128, b), (M, b - 128, b), ("X2S", b - 128, b), ALU.max)
        cur[0] = "o"
        scatter(("XT", 0, 12288), (OF, 0, 8), (V, 0, 128))
        scatter(("BT", 512, 12800), (OF, 0, 8), (C, 0, 128))
        cur[0] = "z"
        scatter(("BT", 512, 12800), ("OIN%d" % t, 0, 24), ("CIN%d" % t, 0, 384))
        scatter(("XT", 0, 12288), ("OIN%d" % t, 0, 24), ("VIN%d" % t, 0, 384))
        for m in ORDER:
            out = ("C%d" % (t + 1), 128 * m, 128 * m + 128) if t + 1 < NR else ("YC", m, 512, 4)
            gather(out, ("BT", 0, 4608), (NX, 8 * m, 8 * m + 8))

    cur[0] = "st"
    dma("Y", "stx", T.yx[:], ("XT", 0, 4096), 5.5)
    dma("Y", "stc", T.yc[:], ("YC", 0, 512), 3.0)
    run_queues(g, T, ops, sent)


def schedule(ops):
    n = len(ops)
    users = [[] for _ in range(n)]
    for i, o in enumerate(ops):
        for j in o["deps"]:
            users[j].append(i)
    prio = [0.0] * n
    for i in range(n - 1, -1, -1):
        prio[i] = min(d for d, _ in ops[i]["alts"].values()) + ops[i]["lat"] + max([prio[u] + WAKE for u in users[i]] or [0.0])
    prio = [p + BON.get(o["tag"], 0.0) for p, o in zip(prio, ops)]
    left = [len(o["deps"]) for o in ops]
    ready = [0.0] * n
    free = {q: 0.0 for o in ops for q in o["alts"]}
    cand = [i for i in range(n) if left[i] == 0]
    seq = []
    while cand:
        s, q = min((max(ready[i], free[q]), q) for i in cand for q in ops[i]["alts"])
        pick = max((i for i in cand if q in ops[i]["alts"] and max(ready[i], free[q]) <= s + LOOK),
                   key=lambda i: (prio[i], -i))
        o = ops[pick]
        dur = o["alts"][q][0]
        st = max(ready[pick], free[q])
        if q != "N":
            free[q] = st + dur
        cand.remove(pick)
        seq.append((pick, q))
        for u in users[pick]:
            ready[u] = max(ready[u], st + dur + (o["lat"] + WAKE if ops[u]["deps"][pick] else 0.0))
            left[u] -= 1
            if left[u] == 0:
                cand.append(u)
    return seq


def improve(ops, seq):
    n = len(ops)
    order, qof = [i for i, q in seq], [None] * n
    for i, q in seq:
        qof[i] = q
    users = [set() for _ in range(n)]
    above = [set() for _ in range(n)]
    hard = [[] for _ in range(n)]
    for i, o in enumerate(ops):
        for j in sorted(o["deps"], reverse=True):
            users[j].add(i)
            if o["deps"][j] and j not in above[i]:
                hard[i].append(j)
                above[i] |= above[j] | {j}
    durs = [[{q: d + o["ind"] * (r - 1) for q, (d, _) in o["alts"].items()} for o in ops] for r in RATES]
    lat = [o["lat"] + WAKE for o in ops]
    heads = [i for i, o in enumerate(ops) if o["tag"] == "cin" and "G" in o["alts"]]
    size = heads[1] - heads[0]
    first, last = heads[0], heads[0] + NR * size
    marks = [{i: 0.0 for i in range(first + size - 4, last, size)} for r in RATES]
    ends = [[0.0] * n for r in RATES]

    def clock(slack):
        for dur, end, mark in zip(durs, ends, marks):
            free = {"G": 0.0, "P": 0.0, "S": 0.0, "V": 0.0, "Y": 0.0, "N": 0.0}
            for i in order:
                q = qof[i]
                st = free[q]
                for j in hard[i]:
                    e = end[j] - NEAR if qof[j] == q else end[j]
                    if e > st:
                        st = e
                st += dur[i][q]
                if q != "N":
                    free[q] = st
                end[i] = st + lat[i]
                if i in mark and st > mark[i] + slack:
                    return 1e9
        return sum(max(end) for end in ends) / len(ends)

    def remember():
        for end, mark in zip(ends, marks):
            mark.update({i: end[i] - lat[i] for i in mark})

    def critical(dur, end):
        start = [end[i] - lat[i] - dur[i][qof[i]] for i in range(n)]
        order.sort(key=lambda i: start[i])
        before, seen = {}, {}
        for i in order:
            before[i], seen[qof[i]] = seen.get(qof[i]), i
        path = [end.index(max(end))]
        while start[path[-1]] > 1e-6:
            i = path[-1]
            near = hard[i] + ([before[i]] if before[i] is not None and qof[i] != "N" else [])
            path.append(max(near, key=lambda j: end[j] - (lat[j] if j not in hard[i] else NEAR if qof[j] == qof[i] else 0)))
        return path

    def move(i, j, behind, q):
        p, r = order.index(i), order.index(j)
        to = r + behind - (r > p)
        if any(x in ops[i]["deps"] for x in order[to:p]) or any(x in users[i] for x in order[p + 1:to + 1]):
            return []
        was, qof[i] = qof[i], q
        order.insert(to, order.pop(p))
        return [(i, p, to, was)]

    now = clock(1e9)
    best = (now, list(order), list(qof))
    for it, (r0, r1, r2, r3, r4, r5, r6) in enumerate(np.random.RandomState(SEED).random_sample((MOVES, 7)).tolist()):
        if it % 50 == 0:
            clock(1e9)
            remember()
            path = critical(durs[it // 50 % len(RATES)], ends[it // 50 % len(RATES)])
        p = order.index(path[int(r1 * len(path))]) if r0 < 0.6 else int(r1 * n)
        if r0 < 0.3:
            p = min(n - 1, max(0, p + int(r0 * 80) - 12))
        i, span = order[p], (4, 10, 25, 60)[int(r2 * 4)]
        q = qof[i]
        if len(ops[i]["alts"]) > 1 and r3 < 0.4:
            q = "S" if q == "V" else "V"
        a = b = p
        while a > 0 and p - a < span and order[a - 1] not in ops[i]["deps"]:
            a -= 1
        while b < n - 1 and b - p < span and order[b + 1] not in users[i]:
            b += 1
        to = a + int(r4 * (b - a + 1))
        if to == p and (p == 0 or q == qof[i]):
            continue
        j, behind = (order[to], to > p) if to != p else (order[p - 1], True)
        done = move(i, j, behind, q)
        if r6 < TWINS and first <= i < last and first <= j < last:
            for d in range(-2 * size, 3 * size, size):
                if d and first <= i + d < last and first <= j + d < last:
                    done += move(i + d, j + d, behind, q)
        slack = -(HEAT * (1 - it / MOVES) + 0.003) * math.log(r5 + 1e-12)
        total = clock(len(RATES) * slack + 0.3)
        if total <= now + slack:
            now = total
            remember()
            if now < best[0]:
                best = (now, list(order), list(qof))
        else:
            for i, p, to, was in reversed(done):
                order.insert(p, order.pop(to))
                qof[i] = was
    return [(i, best[2][i]) for i in best[1]]


def run_queues(g, T, ops, sent):
    eng = {"V": g.vector, "S": g.scalar, "P": g.tensor, "G": g, "Y": g.sync}
    cnt = {"V": 0, "S": 0, "P": 0, "G": 0}
    clock = {q: {} for q in eng}
    know, done = {}, {}
    if not PLAN:
        PLAN.extend(improve(ops, schedule(ops)))
    for i, q in PLAN:
        o = ops[i]
        if q == "N":
            know[i] = {o["sem"]: o["val"]}
            done[i] = (o["sem"], o["val"])
            continue
        ck = clock[q]
        need = {}
        for j, hard in o["deps"].items():
            if hard:
                sem, val = done[j]
                if sem not in need or need[sem][0] < val:
                    need[sem] = (val, j)
        for sem, (val, j) in sorted(need.items(), key=lambda e: -e[1][1]):
            if ck.get(sem, 0) >= val:
                continue
            eng[q].wait_ge(T.sem[sem], val)
            for s2, v2 in know[j].items():
                ck[s2] = max(ck.get(s2, 0), v2)
        if q == "G" and ck.get("qG", 0) < cnt[q]:
            g.wait_ge(T.sem.qG, cnt[q])
            ck["qG"] = cnt[q]
        ins = o["alts"][q][1]()
        if o["sem"]:
            ins.then_inc(T.sem[o["sem"]], 16)
        elif ins is not None:
            cnt[q] += 1
            ins.then_inc(T.sem["q" + q], 1)
        know[i] = dict(ck)
        done[i] = (o["sem"], o["val"]) if o["sem"] else ("q" + q, cnt.get(q, 0))
        know[i][done[i][0]] = done[i][1]
    for q in sorted(cnt):
        g.wait_ge(T.sem["q" + q], cnt[q])
    g.wait_ge(T.sem.loc, sent[0])
    for s in DMAS:
        g.wait_ge(T.sem[s], 16)
